import numpy as np, ml_dtypes
CORES = [40,41,42,43,44,45,46,47]
N = 8
BF = ml_dtypes.bfloat16
def gentries(a):
    return np.ascontiguousarray(a.reshape(8, 16, -1).transpose(0, 2, 1)).reshape(8, -1)
def gtable(e):
    e = np.asarray(e); return np.ascontiguousarray(e.reshape(8, -1, 16).transpose(0, 2, 1)).reshape(128, -1).astype(np.int32)
W, NB, R, H = 2048, 16, 3, 3
KAP = (101, 1303, 2717, 3911)
def spot(u, l):
    return ((u * u >> 5) + 37 * u + KAP[l]) & (W - 1)
def figures(x, n):
    return np.take_along_axis(x, n.reshape(8, 1, -1), 2).reshape((8, 16) + n.shape[1:])
def witness(x, w, F):
    w = w.reshape(8, 16, 1, 1, 1)
    for l in range(4):
        h = F.shape[3] >> 1
        a, b = F[:, :, :, :h], F[:, :, :, h:]
        u = np.add.reduce(w * np.abs(a - b), axis=1) & (W - 1)
        F = figures(x, spot(u, l))
    return F[:, :, :, 0]
def judge(x, w, n):
    F = figures(x, n)
    col = witness(x, w, F); row = witness(x, w, F.transpose(0, 1, 2, 4, 3))
    return col, np.add.reduce(np.abs(col - row), axis=1), np.add.reduce(col, axis=1), np.add.reduce(row, axis=1)
def readings(x, w, n):
    x8 = np.broadcast_to(x, (8, 16, W)); w8 = np.broadcast_to(w, (8, 16))
    return np.ascontiguousarray(witness(x8, w8, figures(x8, n.reshape(8, -1, 16, 1)))[..., 0].transpose(1, 0, 2)).reshape(16, -1)
def parts(rng):
    x = rng.integers(0, 256, (N, 8, 16, W)); w = rng.integers(0, 256, (N, 8, 16)); th = rng.integers(800, 2000, (N, 8, 16))
    return x, w, th, rng.integers(0, W, (N, 8, NB * 256)), rng.integers(0, W, (N, 8, NB * 256))
def pack(x, w, th, b, c):
    return {"xf": np.ascontiguousarray(x.reshape(N, 128, W)).astype(np.float32).astype(BF), "bn": np.stack([gtable(a) for a in b]), "cn": np.stack([gtable(a) for a in c]),
            "wt": np.ascontiguousarray(w.reshape(N, 128, 1)).astype(np.int32), "th": np.ascontiguousarray(th.reshape(N, 128, 1)).astype(np.int32)}
def setup_inputs(rng):
    return pack(*parts(rng))
def setup_inputs_spread(rng):
    x, w, th, b, c = parts(rng)
    s = np.exp2(8.5 * rng.random((N, 8, 1, W))) * (rng.random((N, 8, 1, W)) > 0.0625)
    x = np.minimum((s * rng.random((N, 8, 16, W))).astype(np.int64), 255)
    w = np.minimum(np.exp2(8 * rng.random((N, 8, 16))).astype(np.int64) - rng.integers(0, 2, (N, 8, 16)), 255)
    th = np.minimum(np.exp2(11 * rng.random((N, 8, 16))).astype(np.int64), 4080)
    b = np.minimum((W * rng.random(b.shape) ** 3).astype(np.int64), W - 1); c = np.minimum((W * rng.random(c.shape) ** 2).astype(np.int64), W - 1)
    b[:, 1::2] = W - 1 - b[:, 1::2]; c[:, ::3] = W - 1 - c[:, ::3]
    return pack(x, w, th, b, c)
def setup_inputs_ends(rng):
    x = 255 * rng.integers(0, 2, (N, 8, 16, W)); w = 255 * rng.integers(0, 2, (N, 8, 16)); th = 4080 * rng.integers(0, 2, (N, 8, 16))
    w[:, 0, 0] = 0; w[:, 0, 15] = 255; th[:, 0, 0] = 0; th[:, 0, 15] = 4080
    b, c = [np.where(rng.random((N, 8, NB * 256)) < 0.8, (W - 1) * rng.integers(0, 2, (N, 8, NB * 256)), rng.integers(0, W, (N, 8, NB * 256))) for i in range(2)]
    for g in (2, 5, 7):
        x[:, g] = 255 * rng.integers(0, 2, (N, 1, W)); w[:, g] = 255
    for q in range(0, N - 1, 2): w[q, 7, q] = 0
    for q in range(N):
        for g in (2, 5, 7):
            u = 255 * int(np.add.reduce(w[q, g])) & (W - 1)
            x[q, g, :, 0] = 0; x[q, g, :, W - 1] = 255
            for l in range(4): x[q, g, :, spot(0, l)] = 0
            for l in range(4): x[q, g, :, spot(u, l)] = 255
    bb = b.reshape(N, 8, NB, 16, 16)
    bb[:, 7, :, :, 0] = 0; bb[:, 7, NB - 1] = 0; bb[:, 7, NB - 1, 0, 15] = W - 1; bb[:, 7, NB - 1, 1, 0] = W - 1
    th[:, 7, 15] = 0; th[N - 1, 7, 15] = 4080
    return pack(x, w, th, bb.reshape(N, 8, NB * 256), c)
def setup_inputs_corners(rng):
    x, w, th, b, c = parts(rng)
    for q in range(N):
        for g in range(8):
            k = (g + q) % 8
            if k == 0: w[q, g] = 0
            if k == 1: w[q, g] = 255
            if k == 2: w[q, g] = 16 * rng.integers(1, 16, 16); th[q, g] = 0
            if k == 3: th[q, g] = 4080
            if k == 4: b[q, g] = np.repeat(rng.choice(np.array([0, 1, W - 1, W >> 1]), NB), 256); c[q, g] = rng.permutation(NB * 256) % W
            if k == 5: b[q, g] = np.arange(NB * 256) % W; c[q, g] = W - 1 - b[q, g]
            if k == 6: w[q, g] = 0; w[q, g, 15] = 255
            if k == 7: x[q, g] = 255 * rng.integers(0, 2, (1, W))
    return pack(x, w, th, b, c)
def setup_inputs_full(rng):
    x, w, th, b, c = parts(rng); bb = b.reshape(N, 8, NB, 16, 16); z = spot(0, 3)
    for q in range(N):
        for g in range(8):
            k = (g + q) % 8
            if k < 4: th[q, g] = rng.integers(0, 256, 16)
            if k < 3:
                w[q, g, 0] |= 1; x[q, g, :, z] = rng.integers(240, 256, 16)
                n = rng.integers(0, W, (512, 16)); f = readings(x[q, g], w[q, g], n)
                s = np.add.reduce(f, axis=0); d = np.add.reduce(w[q, g][:, None] * f, axis=0) & (NB - 1)
                for v, p in enumerate(rng.permutation(NB)):
                    turn = k == 1 or (k == 2 and p % 2 == 1)
                    i = int(np.argmax(np.where(d == v, -s if turn else s, -5000)))
                    bb[q, g, p] = n[i][:, None] if turn else rng.integers(0, W, (1, 16))
                    bb[q, g, p, :, 0] = n[i]
            if k == 3:
                w[q, g] = 255; x[q, g, :, z] = 255; x[q, g, rng.permutation(16)[:2 + q], z] = 254
                bb[q, g, :, :, 0] = rng.integers(0, W, (NB, 1))
            if k == 4: x[q, g] = rng.integers(235, 256, (16, W)); w[q, g] = rng.integers(253, 256, 16)
            if k == 7: x[q, g] = rng.integers(246, 256, (16, W)); w[q, g] = rng.integers(240, 256, 16)
            if k == 5 or k == 6:
                e = int(rng.choice(np.array([8, 24, 60, 90])))
                x[q, g] = np.abs(255 * rng.integers(0, 2, (1, W)) - rng.integers(0, e + 1, (16, W))); w[q, g] = rng.integers(240, 256, 16)
        col, D, A, E = judge(x[q], w[q], bb[q])
        i = np.argmax(np.where(D >= 2304, rng.random(D.shape), -1.0), axis=1)
        t = np.take_along_axis(D - (A & 15), i[:, None, :], 1)[:, 0] - rng.integers(0, 2, (8, 16))
        for g in range(8):
            k = (g + q) % 8
            if k > 3: th[q, g] = np.minimum(np.maximum(t[g], 0), 4080)
            if k == 4 or k == 7: th[q, g, ::2] = rng.integers(0, 16, 8)
    return pack(x, w, th, bb.reshape(N, 8, NB * 256), c)
def setup_inputs_ties(rng):
    x, w, th, b, c = parts(rng)
    base = rng.integers(0, 256, (N, 16, 1)); order = np.argsort(rng.random((N, 16, W)), axis=1)
    x[:, 6] = np.take_along_axis(np.ascontiguousarray(np.broadcast_to(base, (N, 16, W))), order, 1)
    x[:, 4, :, 1::2] = x[:, 4, :, 0::2]
    bb = b.reshape(N, 8, NB, 16, 16)
    s = bb[:, 1, ::3].copy(); bb[:, 1, ::3] = np.triu(s) + np.swapaxes(np.triu(s, 1), -1, -2)
    bb[:, 2, :, :, 0] = bb[:, 2, :1, :, 0].copy()
    for q in range(N):
        col, D, A, E = judge(x[q], w[q], bb[q])
        v = np.take_along_axis(D - (A & 15), rng.integers(0, NB, (8, 1, 16)), 1)[:, 0]
        th[q] = np.minimum(np.maximum(v + rng.choice(np.array([-1, 0, 0, 1]), (8, 16)), 0), 4080)
    th[:, 6, 1::2] = 0
    return pack(x, w, th, bb.reshape(N, 8, NB * 256), c)
def check_inputs(d):
    bad = []
    for k, lo, hi in (("xf", 0, 255), ("bn", 0, W - 1), ("cn", 0, W - 1), ("wt", 0, 255), ("th", 0, 4080)):
        v = np.asarray(d[k]).astype(np.float64)
        if not (np.min(v) >= lo and np.max(v) <= hi): bad.append("range of " + k)
        if np.any(v != np.floor(v)): bad.append("whole numbers of " + k)
    return bad
def reference(xf, bn, cn, wt, th):
    x = np.asarray(xf).astype(np.float32).astype(np.int64).reshape(N, 8, 16, W); w = wt.astype(np.int64).reshape(N, 8, 16); lim = th.astype(np.int64).reshape(N, 8, 16)
    b = np.stack([gentries(a) for a in bn]).astype(np.int64).reshape(N, 8, NB, 16, 16)
    c = np.stack([gentries(a) for a in cn]).astype(np.int64).reshape(N, 8, NB, 16, 16)
    cnt = np.zeros((N, 8, NB, 16), np.int64); low = np.tril(np.ones((NB, NB), bool), -1)
    for t in range(R):
        for a in range(N):
            q = (a - H * t) % N
            col, D, A, E = judge(x[a], w[a], b[q])
            qr = D > lim[a][:, None, :] + (A & 15); cnt[a] += qr
            d = np.add.reduce(w[a][:, :, None] * col[:, :, :, 0], axis=1) & (NB - 1)
            act = ~np.any((d[:, :, None] == d[:, None, :]) & low, axis=2)
            for g in range(8):
                for k in np.flatnonzero(act[g]):
                    one, two = b[q, g, k], c[a, g, d[g, k]]
                    j = np.flatnonzero(qr[g, k] & (A[g, k] <= E[g, k])); v = one[:, j]; one[:, j] = two[:, j]; two[:, j] = v
                    j = np.flatnonzero(qr[g, k] & (A[g, k] > E[g, k])); v = one[j]; one[j] = two[j]; two[j] = v
    yb = np.stack([gtable(b[(a - H * (R - 1)) % N].reshape(8, -1)) for a in range(N)]); yc = np.stack([gtable(e.reshape(8, -1)) for e in c])
    return {"yb": yb.astype(np.float32), "yc": yc.astype(np.float32), "yq": np.ascontiguousarray(cnt.transpose(0, 1, 3, 2)).reshape(N, 128, NB).astype(np.float32)}

@@ -1,0 +1,412 @@
+import numpy as np
+from concourse.mybir import dt, AluOpType, AxisListType, ActivationFunctionType
+import comms_topo
+
+OP = AluOpType
+AF = ActivationFunctionType
+R, NB, HOP = 3, 16, 3
+KAP = (101, 1303, 2717, 3911)
+W = 2048
+
+SCRATCH = {
+    "xw": ("sbuf", [128, 4096], "bfloat16"),
+    "bni": ("sbuf", [128, 16, 16], "int32"),
+    "cni": ("sbuf", [128, 256], "int32"),
+    "wti": ("sbuf", [128, 1], "int32"),
+    "thi": ("sbuf", [128, 1], "int32"),
+    "cw": ("sbuf", [128, 4096], "float32"),
+    "pi": ("sbuf", [128, 8], "int32"),
+    "pj": ("sbuf", [128, 8], "int32"),
+    "icol": ("sbuf", [128, 8], "float32"),
+    "wcol": ("sbuf", [128, 8], "float32"),
+    "th16": ("sbuf", [128, 8], "float32"),
+    "ones": ("sbuf", [128, 128], "bfloat16"),
+    "m1": ("sbuf", [128, 128], "bfloat16"),
+    "bo": ("sbuf", [128, 128], "bfloat16"),
+    "bo256": ("sbuf", [128, 128], "bfloat16"),
+    "bow": ("sbuf", [128, 128], "bfloat16"),
+    "ident": ("sbuf", [128, 128], "bfloat16"),
+    "nident": ("sbuf", [128, 128], "bfloat16"),
+    "zw": ("sbuf", [128, 144], "bfloat16"),
+    "z1": ("sbuf", [128, 144], "bfloat16"),
+    "z16": ("sbuf", [128, 144], "bfloat16"),
+    "prow": ("sbuf", [128, 128], "float32"),
+    "cmpc": ("sbuf", [128, 256], "float32"),
+    "bli": ("sbuf", [128, 16], "int32"),
+    "bl": ("sbuf", [128, 16], "uint16"),
+    "zero": ("sbuf", [128, 8], "float32"),
+    "oh": ("sbuf", [128, 24], "float32"),
+    "ex": ("sbuf", [128, 16], "float32"),
+    "qs": ("sbuf", [128, 16], "float32"),
+    "qf": ("sbuf", [128, 16], "float32"),
+}
+for _t in range(R):
+    SCRATCH["qr%d" % _t] = ("sbuf", [128, 16], "float32")
+    for _h in range(2):
+        SCRATCH["lt%d%d" % (_t, _h)] = ("sbuf", [128, 128], "uint16")
+        SCRATCH["bn%d%d" % (_t, _h)] = ("sbuf", [128, 128], "float32")
+        SCRATCH["b3%d%d" % (_t, _h)] = ("sbuf", [128, 8, 16], "float32")
+        if _t < R - 1:
+            SCRATCH["ls%d%d" % (_t, _h)] = ("sbuf", [128, 128], "uint16")
+for _h in range(2):
+    for _n, _s, _d in (("fa", [128, 1024], "bfloat16"), ("dc", [128, 1024], "bfloat16"), ("ac", [128, 1024], "bfloat16"),
+                       ("ar", [128, 2, 8, 64], "bfloat16"), ("i1", [128, 128], "int32"), ("i2", [128, 128], "int32"),
+                       ("j0", [128, 16, 8], "int32"), ("j1", [128, 16, 4], "int32"), ("j2", [128, 16, 2], "int32"), ("j3", [128, 2, 8], "int32"),
+                       ("la", [128, 64], "uint16"), ("lb", [128, 64], "uint16"),
+                       ("wc", [128, 128], "bfloat16"), ("da", [128, 2, 128], "bfloat16"),
+                       ("ii", [128, 16], "int32"), ("id", [128, 16], "int32"), ("ce", [128, 8], "bfloat16"),
+                       ("go", [128, 8], "uint16"), ("gf", [128, 8], "float32"), ("sf", [128, 8], "float32"), ("so", [128, 8], "uint16"),
+                       ("tb", [128, 128], "float32"), ("cp", [128, 128], "float32"), ("ms", [128, 128], "float32"),
+                       ("t16", [128, 8], "float32"), ("ta", [128, 8], "float32"), ("qa", [128, 8], "float32"), ("sg", [128, 8], "float32"),
+                       ("zz", [128, 8], "float32"), ("ee", [128, 256], "bfloat16")):
+        SCRATCH["%s_%d" % (_n, _h)] = ("sbuf", _s, _d)
+    for _n in ("S", "F", "X", "Y"):
+        SCRATCH["%s_%d" % (_n, _h)] = ("psum", [128, 512], "float32")
+
+DMAS = ["ld%d" % _k for _k in range(8)] + ["st%d" % _k for _k in range(4)]
+SEMAPHORES = ["V", "A", "P", "G", "sent"] + DMAS + ["%s%d%d" % (_a, _t, _h) for _a in ("al", "ab") for _t in (1, 2) for _h in (0, 1)]
+
+CY = 0.00083
+HOPT = 0.06
+
+
+def cost(q, n):
+    if q == "V":
+        return 0.01 + max(64, n) * CY
+    if q == "A":
+        return 0.03 + max(64, n) * CY
+    if q == "P":
+        return n * 0.00042
+    return 0.2
+
+
+def build(core, T, topo):
+    ops, lastw, readers, banks = [], {}, {}, {}
+
+    def add(q, fn, rd=(), wr=(), bk=(), c=0.1, sem=None, n=1, note=""):
+        deps, order = set(), set()
+        for k in rd:
+            if k in lastw:
+                deps.add(lastw[k])
+        for k in wr:
+            if k in lastw:
+                deps.add(lastw[k])
+            deps.update(readers.get(k, ()))
+        for b in bk:
+            for e, o in banks.get(b, {}).items():
+                if e != q:
+                    deps.add(o)
+                else:
+                    order.add(o)
+        me = len(ops)
+        for k in wr:
+            lastw[k], readers[k] = me, []
+        for k in rd:
+            readers.setdefault(k, []).append(me)
+        for b in bk:
+            banks.setdefault(b, {})[q] = me
+        deps.discard(me)
+        ops.append({"q": q, "fn": fn, "deps": deps, "order": order - deps, "c": c, "sem": sem, "n": n, "note": note})
+        return me
+
+    def V(fn, rd, wr, n, bk=(), note=""):
+        return add("V", fn, rd, wr, bk, cost("V", n), note=note)
+
+    def A(fn, rd, wr, n, bk=(), note=""):
+        return add("A", fn, rd, wr, bk, cost("A", n), note=note)
+
+    def P(fn, rd, wr, n, bk=(), note=""):
+        return add("P", fn, rd, wr, bk, cost("P", n), note=note)
+
+    def G(fn, rd, wr, c, note=""):
+        return add("G", fn, rd, wr, (), c, note=note)
+
+    def load(q, k, out, in_, wr, c):
+        add(q, lambda e: e.dma_start(out, in_), (), wr, (), c, sem="ld%d" % k, n=16, note="load")
+
+    gat = lambda n: int(60 + 1.5 * n)
+
+    load("Y", 0, T.bni[:, :, :], T.bn[:, :], ("bni",), 2.2)
+    load("Q", 1, T.xw[:, 0:W], T.xf[:, :], ("xw",), 4.0)
+    load("Y", 2, T.wti[:, :], T.wt[:, :], ("wti",), 2.5)
+    load("Y", 3, T.thi[:, :], T.th[:, :], ("thi",), 2.5)
+    load("Y", 4, T.xw[:, W:2 * W], T.xf[:, :], ("xw2",), 6.0)
+    load("Q", 5, T.cni[:, :], T.cn[:, :], ("cni",), 6.0)
+
+    G(lambda e: e.iota(T.pi[:, 0:1], [[0, 1]], 0, 1), (), ("pi",), 0.2)
+    G(lambda e: e.iota(T.bli[:, :], [[0, 2], [1, 8]], 0, 0), (), ("bli",), 0.2)
+    G(lambda e: e.iota(T.prow[:, :], [[0, 8], [1, 16]], 0, 0, allow_small_or_imprecise_dtypes=True), (), ("prow",), 0.4)
+    V(lambda e: e.memset(T.ones[:, :], 1.0), (), ("ones",), 128)
+    G(lambda e: e.affine_select(T.ident[:, :], T.ones[:, :], [[-1, 128]], OP.is_equal, 0.0, 0, 1), ("ones",), ("ident",), 0.4)
+    G(lambda e: e.affine_select(T.m1[:, :], T.ones[:, :], [[-16, 8], [0, 16]], OP.is_ge, 0.0, 0, 1), ("ones",), ("m1",), 0.4)
+    G(lambda e: e.affine_select(T.bo[:, :], T.m1[:, :], [[16, 8], [0, 16]], OP.is_ge, 0.0, 15, -1), ("m1",), ("bo",), 0.4)
+    V(lambda e: e.memset(T.zw[:, :], 0.0), (), ("zw",), 144)
+    V(lambda e: e.memset(T.z1[:, :], 0.0), (), ("z1",), 144)
+    V(lambda e: e.memset(T.z16[:, :], 0.0), (), ("z16",), 144)
+    V(lambda e: e.memset(T.zero[:, :], 0.0), (), ("zero",), 8)
+    V(lambda e: e.memset(T.oh[:, 0:1], 0.0), (), ("ohz",), 8)
+
+    def lists_in(h):
+        for ph in range(2):
+            V(lambda e, ph=ph: e.tensor_copy(T["lt0%d" % h][:, 64 * ph:64 * ph + 64], T.bni[:, 8 * h:8 * h + 8, 8 * ph:8 * ph + 8]),
+              ("bni",), ("lt0%d%d" % (h, ph),), 64)
+
+    def charts_in(h):
+        V(lambda e: e.tensor_copy(T["bn0%d" % h][:, :], T.bni[:, 8 * h:8 * h + 8, :]), ("bni",), ("bn0%d" % h,), 128)
+    lists_in(0)
+    V(lambda e: e.tensor_scalar(T.nident[:, :], T.ident[:, :], -1.0, None, OP.mult), ("ident",), ("nident",), 64)
+    V(lambda e: e.tensor_copy(T.wcol[:, 0:1], T.wti[:, :]), ("wti",), ("wcol",), 8)
+    V(lambda e: e.tensor_scalar(T.zw[:, 15:128:16], T.bo[:, 0:128:16], T.wcol[:, 0:1], None, OP.mult), ("bo", "wcol"), ("zw",), 8)
+    lists_in(1)
+    V(lambda e: e.tensor_scalar(T.th16[:, 0:1], T.thi[:, :], 0.0625, None, OP.mult), ("thi",), ("th16",), 8)
+    V(lambda e: e.tensor_scalar(T.pj[:, 0:1], T.pi[:, 0:1], 15, None, OP.bitwise_and), ("pi",), ("pj",), 8)
+    V(lambda e: e.tensor_copy(T.icol[:, 0:1], T.pj[:, 0:1]), ("pj",), ("icol",), 8)
+    V(lambda e: e.tensor_copy(T.bl[:, :], T.bli[:, :]), ("bli",), ("bl",), 16)
+    V(lambda e: e.tensor_copy(T.z1[:, 15:128:16], T.bo[:, 0:128:16]), ("bo",), ("z1",), 8)
+    V(lambda e: e.tensor_scalar(T.z16[:, 15:128:16], T.bo[:, 0:128:16], 0.0625, None, OP.mult), ("bo",), ("z16",), 8)
+    V(lambda e: e.tensor_scalar(T.bow[:, :], T.bo[:, :], T.wcol[:, 0:1], None, OP.mult), ("bo", "wcol"), ("bow",), 64)
+    V(lambda e: e.tensor_scalar(T.bo256[:, :], T.bo[:, :], 256.0, None, OP.mult), ("bo",), ("bo256",), 64)
+    V(lambda e: e.memset(T.cmpc[:, 128:256], -0.25), (), ("cmpc",), 128)
+    V(lambda e: e.tensor_scalar(T.cmpc[:, 0:128], T.prow[:, :], T.icol[:, 0:1], 0.25, OP.not_equal, OP.add), ("prow", "icol"), ("cmpc2",), 128)
+    charts_in(0)
+    charts_in(1)
+    V(lambda e: e.tensor_copy(T.cw[:, 0:256], T.cni[:, :]), ("cni",), ("cw",), 256)
+
+    def half(t, h):
+        B = lambda n: T["%s_%d" % (n, h)]
+        K = lambda n: "%s_%d" % (n, h)
+        S, F, X, Y = B("S"), B("F"), B("X"), B("Y")
+        lt, bn = T["lt%d%d" % (t, h)], T["bn%d%d" % (t, h)]
+        win = T.xw[:, 0:W]
+        fa, dc, ac, ar = B("fa"), B("dc"), B("ac"), B("ar")
+        zs = lambda z, i: z[:, 15 - i:143 - i]
+
+        def gather_pair(la, lb, ka, kb, n, w, wk, ch):
+            m = n // ch
+            for c in range(ch):
+                A(lambda e, c=c: e.activation(fa[:, m * c:m * c + m], w.indirect(la[:, m * c // 16:(m * c + m) // 16]), AF.Identity),
+                  ka + wk, (K("fa%d" % c),), gat(m), note="gA")
+            for c in range(ch):
+                V(lambda e, c=c: e.tensor_tensor(dc[:, m * c:m * c + m], w.indirect(lb[:, m * c // 16:(m * c + m) // 16]), fa[:, m * c:m * c + m], OP.subtract),
+                  kb + wk + (K("fa%d" % c),), (K("dc%d" % c),), gat(m), note="gB")
+            for c in range(ch):
+                A(lambda e, c=c: e.activation(ac[:, m * c:m * c + m], dc[:, m * c:m * c + m], AF.Abs), (K("dc%d" % c),), (K("ac%d" % c),), m, note="abs")
+            return tuple(K("fa%d" % c) for c in range(ch)), tuple(K("dc%d" % c) for c in range(ch)), tuple(K("ac%d" % c) for c in range(ch))
+
+        def weigh(out, n, keys, wr):
+            def fn(e):
+                for i in range(16):
+                    o = e.matmul(out, zs(T.zw, i), ac[:, i:16 * n:16], i == 0, i == 15)
+                return o
+            P(fn, keys + ("zw",), wr, 16 * max(64, n), (K("S"),), note="weigh")
+
+        def index(l, n):
+            i1, i2, j = B("i1"), B("i2"), B("j%d" % l)
+            full = j[:, :, :]
+            V(lambda e: e.tensor_copy(i1[:, 0:n], S[:, 0:n]), (K("S"),), (K("i1"),), n, (K("S"),), note="i1")
+            V(lambda e: e.tensor_scalar(i2[:, 0:n], i1[:, 0:n], W - 1, None, OP.bitwise_and), (K("i1"),), (K("i2"),), n, note="i2")
+            V(lambda e: e.tensor_scalar(S[:, 256:256 + n], i2[:, 0:n], 1184.0, None, OP.add), (K("i2"),), (K("Su"),), n, (K("S"),), note="i3")
+            V(lambda e: e.tensor_tensor(i1[:, 0:n], i2[:, 0:n], S[:, 256:256 + n], OP.mult), (K("i2"), K("Su")), (K("i1"),), n, (K("S"),), note="i4")
+            V(lambda e: e.tensor_scalar(full, i1[:, 0:n], 5, W - 1, OP.arith_shift_right, OP.bitwise_and), (K("i1"),), (K("j"),), n, note="i5")
+            k = KAP[l] % W
+            r = k % 16
+            la, lb = B("la"), B("lb")
+            h2 = n // 2
+            m = n // 16
+            for x, (o, key) in enumerate(((la, "la"), (lb, "lb"))):
+                src = j[:, :, x * (m // 2):(x + 1) * (m // 2)] if l < 3 else j[:, x, :]
+                V(lambda e, o=o, src=src: e.tensor_scalar(o[:, 0:h2], src, float(r), None, OP.add), (K("j"),), (K(key),), h2, note="i6")
+            a = k - r
+            return T.xw[:, a:a + W + 16]
+
+        fk, dk, ak = gather_pair(lt[:, 0:64], lt[:, 64:128], ("lt%d%d0" % (t, h),), ("lt%d%d1" % (t, h),), 1024, win, ("xw",), 2)
+
+        def rows(bank, srcs):
+            def fn(e):
+                for c in range(8):
+                    lst = [(T.ident, s[:, c:1024:16]) for s in srcs] + [(T.nident, s[:, c + 8:1024:16]) for s in srcs]
+                    for i, (w, r) in enumerate(lst):
+                        o = e.matmul(bank[:, c:512:8], w[:, :], r, i == 0, i == len(lst) - 1)
+                return o
+            return fn
+        P(rows(X, (fa,)), fk + ("ident", "nident"), (K("X"),), 1024, (K("X"),), note="row0")
+        P(rows(Y, (fa, dc)), fk + dk + ("ident", "nident"), (K("Y"),), 2048, (K("Y"),), note="row1")
+        for ph, (bank, kk) in enumerate(((X, K("X")), (Y, K("Y")))):
+            A(lambda e, ph=ph, bank=bank: e.activation(ar[:, ph, :, :], bank[:, :], AF.Abs), (kk,), (K("ar%d" % ph),), 512, (kk,), note="absr")
+        weigh(S[:, 0:64], 64, ak, (K("S"),))
+
+        def wrow(e):
+            for ph in range(2):
+                for pl in range(8):
+                    o = e.matmul(S[:, 64:128], zs(T.zw, 8 * ph + pl), ar[:, ph, :, 8 * pl:8 * pl + 8], ph + pl == 0, 8 * ph + pl == 15)
+            return o
+        P(wrow, ("zw", K("ar0"), K("ar1")), (K("S"),), 1024, (K("S"),), note="weighr")
+        w = index(0, 128)
+        for l, n in ((1, 1024), (2, 512), (3, 256)):
+            fk, dk, ak = gather_pair(B("la"), B("lb"), (K("la"),), (K("lb"),), n, w, ("xw", "xw2"), 2 if n > 600 else 1)
+            weigh(S[:, 0:n // 16], n // 16, ak, (K("S"),))
+            w = index(l, n // 16)
+        wc, da, ii, id_ = B("wc"), B("da"), B("ii"), B("id")
+        wk = ("xw", "xw2")
+        A(lambda e: e.activation(wc[:, :], w.indirect(B("la")[:, 0:8]), AF.Identity), wk + (K("la"),), (K("wc"),), gat(128), note="gWC")
+        V(lambda e: e.tensor_tensor(da[:, 0, :], w.indirect(B("lb")[:, 0:8]), wc[:, :], OP.subtract), wk + (K("lb"), K("wc")), (K("dw"),), gat(128), note="gWR")
+        A(lambda e: e.activation(da[:, 1, :], da[:, 0, :], AF.Abs), (K("dw"),), (K("aw"),), 128, note="absW")
+        P(lambda e: e.matmul(F[:, 0:8], T.bow[:, :], wc[:, 0:128:16], True, True), (K("wc"), "bow"), (K("Fd"),), 64, (K("F"),), note="donor")
+
+        def asum(e):
+            for i in range(16):
+                o = e.matmul(F[:, 8:16], zs(T.z1, i), wc[:, i:128:16], i == 0, i == 15)
+            return o
+        P(asum, (K("wc"), "z1"), (K("Fa"),), 1024, (K("F"),), note="A")
+        V(lambda e: e.tensor_copy(ii[:, :], F[:, 0:16]), (K("Fd"), K("Fa")), (K("ii"),), 16, (K("F"),), note="f1")
+        V(lambda e: e.tensor_scalar(id_[:, :], ii[:, :], 15, None, OP.bitwise_and), (K("ii"),), (K("id"),), 16, note="f2")
+        V(lambda e: e.tensor_scalar(T.oh[:, 8 * h + 1:8 * h + 9], id_[:, 0:8], T.icol[:, 0:1], None, OP.is_equal), (K("id"), "icol"), ("oh%d" % h,), 8, note="oh")
+        V(lambda e: e.tensor_tensor_scan(T.ex[:, 8 * h:8 * h + 8], T.oh[:, 8 * h:8 * h + 8], T.zero[:, 0:8], T.ex[:, 7:8] if h else 0.0, OP.add, OP.add),
+          ("ohz", "oh0", "zero") + (("oh1", "ex0") if h else ()), ("ex%d" % h,), 8, note="scan")
+        V(lambda e: e.tensor_tensor(B("ce")[:, :], T.oh[:, 8 * h + 1:8 * h + 9], T.ex[:, 8 * h:8 * h + 8], OP.mult), ("oh%d" % h, "ex%d" % h), (K("ce"),), 16, note="ce")
+        P(lambda e: e.matmul(F[:, 32:40], T.bo256[:, :], B("ce")[:, :], True, True), (K("ce"), "bo256"), (K("Fc"),), 64, (K("F"),), note="cnt")
+        V(lambda e: e.tensor_scalar(B("go")[:, :], id_[:, 0:8], 16.0, T.icol[:, 0:1], OP.mult, OP.add), (K("id"), "icol"), (K("go"),), 8, note="go")
+        V(lambda e: e.tensor_scalar(B("t16")[:, :], id_[:, 8:16], 0.0625, T.th16[:, 0:1], OP.mult, OP.add), (K("id"), "th16"), (K("t16"),), 8, note="t16")
+        V(lambda e: e.tensor_tensor(B("tb")[:, :], T.cw[:, 0:256].indirect(B("go")[:, :]), bn[:, :], OP.subtract), ("cw", K("go"), "bn%d%d" % (t, h)), (K("tb"),), gat(128), note="T")
+        V(lambda e: e.tensor_tensor(B("ta")[:, :], B("t16")[:, :], F[:, 32:40], OP.add), (K("t16"), K("Fc")), (K("ta"),), 8, (K("F"),), note="ta")
+
+        def dsum(e):
+            for i in range(16):
+                o = e.matmul(S[:, 384:400], zs(T.z16, i), da[:, :, i:128:16], i == 0, i == 15)
+            return o
+        P(dsum, (K("dw"), K("aw"), "z16"), (K("Sd"),), 1024, (K("S"),), note="D")
+        V(lambda e: e.tensor_scalar(B("sg")[:, :], S[:, 384:392], 0.0, 0.5, OP.is_lt, OP.subtract), (K("Sd"),), (K("sg"),), 8, (K("S"),), note="sg")
+        V(lambda e: e.tensor_tensor(B("qa")[:, :], S[:, 392:400], B("ta")[:, :], OP.is_gt), (K("Sd"), K("ta")), (K("qa"),), 8, (K("S"),), note="qa")
+        V(lambda e: e.tensor_tensor(B("zz")[:, :], B("sg")[:, :], B("qa")[:, :], OP.mult), (K("sg"), K("qa")), (K("zz"),), 16, note="zz")
+        V(lambda e: e.tensor_tensor(B("ee")[:, :], B("zz")[:, 0:8].indirect(T.bl[:, :]), T.cmpc[:, :], OP.is_ge), (K("zz"), "bl", "cmpc", "cmpc2"), (K("ee"),), gat(256), note="ee")
+
+        def xm(e):
+            e.matmul(X[:, 0:128], T.bo[:, :], B("ee")[:, 0:128], True, False)
+            return e.matmul(X[:, 0:128], T.ident[:, :], B("ee")[:, 128:256], False, True)
+        P(xm, (K("ee"), "bo", "ident"), (K("X"),), 256, (K("X"),), note="X")
+        A(lambda e: e.activation(Y[:, 0:128], X[:, 0:128], AF.Square, bias=-1.0), (K("X"),), (K("Y"),), 128, (K("X"), K("Y")), note="M")
+        V(lambda e: e.tensor_tensor(Y[:, 128:256], B("tb")[:, :], Y[:, 0:128], OP.mult), (K("tb"), K("Y")), (K("MT"),), 128, (K("Y"),), note="MT")
+        b3 = T["b3%d%d" % (t, h)]
+        kb3 = "b3%d%d" % (t, h)
+        V(lambda e: e.tensor_tensor(b3[:, :, :], bn[:, :], Y[:, 128:256], OP.add), ("bn%d%d" % (t, h), K("MT")), (kb3,), 128, (K("Y"),), note="B")
+        if t < R - 1:
+            ls = T["ls%d%d" % (t, h)]
+            for ph in range(2):
+                V(lambda e, ph=ph: e.tensor_copy(ls[:, 64 * ph:64 * ph + 64], b3[:, :, 8 * ph:8 * ph + 8]), (kb3,), ("ls%d%d%d" % (t, h, ph),), 64, note="ls")
+            dst = T.cores[(T.rank_of(core) + HOP) % len(T.cores)]
+            rid, pid, _ = topo.addr(dst)
+            mask = 0
+            for en in topo.engines(core, dst)[::2]:
+                mask |= 1 << en
+            ne = len(topo.engines(core, dst)[::2])
+            o = add("G", lambda e: e.remote_dma(T["lt%d%d" % (t + 1, h)][:, :], ls[:, :], T.sem["al%d%d" % (t + 1, h)], T.sem["sent"], pid, rid, mask),
+                    ("ls%d%d0" % (t, h), "ls%d%d1" % (t, h)), (), (), 0.3, sem="-sent", n=ne, note="send")
+            arr = add(None, None, (), ("lt%d%d0" % (t + 1, h), "lt%d%d1" % (t + 1, h)), (), 2.0, sem="al%d%d" % (t + 1, h), n=ne)
+            ops[arr]["order"].add(o)
+            o = add("G", lambda e: e.remote_dma(T["bn%d%d" % (t + 1, h)][:, :], b3[:, :, :], T.sem["ab%d%d" % (t + 1, h)], T.sem["sent"], pid, rid, mask),
+                    (kb3,), (), (), 0.3, sem="-sent", n=ne, note="send2")
+            arr = add(None, None, (), ("bn%d%d" % (t + 1, h),), (), 2.5, sem="ab%d%d" % (t + 1, h), n=ne)
+            ops[arr]["order"].add(o)
+        else:
+            add("Y", lambda e: e.dma_start(T.yb[:, 128 * h:128 * h + 128], b3[:, :, :]), (kb3,), (), (), 2.0, sem="st%d" % h, n=16)
+        A(lambda e: e.activation(B("cp")[:, :], T.cw[:, 0:256].indirect(B("go")[:, :]), AF.Identity), ("cw", K("go")), (K("cp"),), gat(128), note="CP")
+        A(lambda e: e.activation(B("ms")[:, :], Y[:, 128:256], AF.Identity), (K("MT"),), (K("ms"),), 128, (K("Y"),), note="MS")
+        V(lambda e: e.tensor_scalar(B("gf")[:, :], id_[:, 0:8], 16.0, T.icol[:, 0:1], OP.mult, OP.add), (K("id"), "icol"), (K("gf"),), 8, note="gf")
+        V(lambda e: e.tensor_tensor(B("sf")[:, :], B("gf")[:, :], F[:, 32:40], OP.add), (K("gf"), K("Fc")), (K("sf"),), 8, (K("F"),), note="sf")
+        V(lambda e: e.tensor_copy(B("so")[:, :], B("sf")[:, :]), (K("sf"),), (K("so"),), 8, note="so")
+        V(lambda e: e.tensor_tensor(T.cw[:, :].indirect(B("so")[:, :]), B("cp")[:, :], B("ms")[:, :], OP.subtract), (K("cp"), K("ms"), K("so")), ("cw",), 60 + 4 * 128, note="scatter")
+        V(lambda e: e.tensor_tensor(T["qr%d" % t][:, 8 * h:8 * h + 8], S[:, 392:400], B("t16")[:, :], OP.is_gt), (K("Sd"), K("t16")), ("qr%d%d" % (t, h),), 8, (K("S"),), note="qr")
+
+    for t in range(R):
+        for h in range(2):
+            half(t, h)
+        if t == 1:
+            V(lambda e: e.tensor_tensor(T.qs[:, :], T.qr0[:, :], T.qr1[:, :], OP.add), ("qr00", "qr01", "qr10", "qr11"), ("qs",), 32)
+    V(lambda e: e.tensor_tensor(T.qf[:, :], T.qs[:, :], T.qr2[:, :], OP.add), ("qs", "qr20", "qr21"), ("qf",), 32)
+    add("Y", lambda e: e.dma_start(T.yq[:, :], T.qf[:, :]), ("qf",), (), (), 2.0, sem="st2", n=16)
+    add("Q", lambda e: e.dma_start(T.yc[:, :], T.cw[:, 0:256]), ("cw",), (), (), 2.0, sem="st3", n=16)
+    return ops
+
+
+def schedule(ops):
+    n = len(ops)
+    tail = [0.0] * n
+    succ = [[] for _ in range(n)]
+    for i, o in enumerate(ops):
+        for d in o["deps"] | o["order"]:
+            succ[d].append(i)
+    for i in range(n - 1, -1, -1):
+        tail[i] = ops[i]["c"] + max([tail[s] + HOPT for s in succ[i]] or [0.0])
+    done, free, left, order, issued = {}, {}, set(range(n)), [], [False] * n
+    isq = lambda i: ops[i]["q"] in ("Y", "Q")
+    while left:
+        best = None
+        for i in left:
+            o = ops[i]
+            if any(d in left for d in o["deps"]) or any(d in left for d in o["order"]):
+                continue
+            r = 0.0
+            for d in o["deps"] | o["order"]:
+                r = max(r, done[d] + (HOPT if d in o["deps"] else 0.0))
+            if o["q"] is not None:
+                r = max(r, free.get(o["q"], 0.0))
+            key = (round(r, 3), -tail[i])
+            if best is None or key < best[0]:
+                best = (key, i, r)
+        _, i, r = best
+        o = ops[i]
+        left.discard(i)
+        done[i] = r + o["c"]
+        if o["q"] is not None:
+            free[o["q"]] = r + (0.06 if isq(i) else o["c"])
+        order.append(i)
+    return order, done
+
+
+_CACHE = {}
+
+
+def rank_program(g, core, T, topo):
+    if T.rank_of(core) is None:
+        return
+    ops = build(core, T, topo)
+    if "order" not in _CACHE:
+        _CACHE["order"] = schedule(ops)
+    order, done = _CACHE["order"]
+    eng = {"V": g.vector, "A": g.scalar, "P": g.tensor, "G": g, "Y": g.sync, "Q": g.scalar}
+    queue = {"V": "V", "A": "A", "Q": "A", "P": "P", "G": "G", "Y": "Y"}
+    total, at, clock = {}, {}, {}
+    known = {q: {} for q in ("V", "A", "P", "G", "Y")}
+    for i in order:
+        o = ops[i]
+        if o["q"] is None:
+            at[i] = (o["sem"], o["n"])
+            clock[i] = {o["sem"]: o["n"]}
+            continue
+        qn = queue[o["q"]]
+        e = eng[o["q"]]
+        kn = known[qn]
+        for d in sorted(o["deps"], key=lambda d: -done[d]):
+            s, c = at[d]
+            if kn.get(s, 0) < c:
+                e.wait_ge(T.sem[s], c)
+                for s2, c2 in clock[d].items():
+                    kn[s2] = max(kn.get(s2, 0), c2)
+        ins = o["fn"](e)
+        if o["sem"] is None:
+            s, n = o["q"], 1
+            total[s] = total.get(s, 0) + n
+            ins.then_inc(T.sem[s], n)
+        elif o["sem"] == "-sent":
+            s = "sent"
+            total[s] = total.get(s, 0) + o["n"]
+        else:
+            s, n = o["sem"], o["n"]
+            total[s] = total.get(s, 0) + n
+            ins.then_inc(T.sem[s], n)
+        at[i] = (s, total[s])
+        clock[i] = dict(kn)
+        clock[i][s] = total[s]
+    for s, c in total.items():
+        if known["G"].get(s, 0) < c:
+            g.wait_ge(T.sem[s], c)

@@ -9,7 +9,12 @@ KAP = (101, 1303, 2717, 3911)
 W = 2048
 
 SCRATCH = {
-    "xw": ("sbuf", [128, 4096], "bfloat16"),
+    "xw": ("sbuf", [128, 2048], "bfloat16"),
+    "tu": ("sbuf", [128, 128], "int32"),
+    "tv": ("sbuf", [128, 128], "int32"),
+    "tf": ("sbuf", [128, 128], "float32"),
+    "tp": ("sbuf", [128, 128], "int32"),
+    "tq": ("sbuf", [128, 128], "int32"),
     "bni": ("sbuf", [128, 16, 16], "int32"),
     "cni": ("sbuf", [128, 256], "int32"),
     "wti": ("sbuf", [128, 1], "int32"),
@@ -35,11 +40,16 @@ SCRATCH = {
     "bli": ("sbuf", [128, 16], "int32"),
     "bl": ("sbuf", [128, 16], "uint16"),
     "zero": ("sbuf", [128, 8], "float32"),
-    "oh": ("sbuf", [128, 24], "float32"),
+    "bo16": ("sbuf", [128, 128], "bfloat16"),
+    "oh": ("sbuf", [128, 24], "bfloat16"),
     "ex": ("sbuf", [128, 16], "float32"),
     "qs": ("sbuf", [128, 16], "float32"),
     "qf": ("sbuf", [128, 16], "float32"),
 }
+SCRATCH["xt"] = ("sbuf", [128, 4 * W], "bfloat16")
+SCRATCH["xa"] = ("sbuf", [128, 512], "int32")
+SCRATCH["xb"] = ("sbuf", [128, 512], "int32")
+SCRATCH["xl"] = ("sbuf", [128, 512], "uint16")
 for _t in range(R):
     SCRATCH["qr%d" % _t] = ("sbuf", [128, 16], "float32")
     for _h in range(2):
@@ -50,12 +60,12 @@ for _t in range(R):
             SCRATCH["ls%d%d" % (_t, _h)] = ("sbuf", [128, 128], "uint16")
 for _h in range(2):
     for _n, _s, _d in (("fa", [128, 1024], "bfloat16"), ("dc", [128, 1024], "bfloat16"), ("ac", [128, 1024], "bfloat16"),
-                       ("ar", [128, 2, 8, 64], "bfloat16"), ("i1", [128, 128], "int32"), ("i2", [128, 128], "int32"),
+                       ("ar", [128, 2, 8, 64], "bfloat16"), ("i1", [128, 128], "int32"),
                        ("j0", [128, 16, 8], "int32"), ("j1", [128, 16, 4], "int32"), ("j2", [128, 16, 2], "int32"), ("j3", [128, 2, 8], "int32"),
                        ("la", [128, 64], "uint16"), ("lb", [128, 64], "uint16"),
                        ("wc", [128, 128], "bfloat16"), ("da", [128, 2, 128], "bfloat16"),
                        ("ii", [128, 16], "int32"), ("id", [128, 16], "int32"), ("ce", [128, 8], "bfloat16"),
-                       ("go", [128, 8], "uint16"), ("gf", [128, 8], "float32"), ("sf", [128, 8], "float32"), ("so", [128, 8], "uint16"),
+                       ("go", [128, 8], "uint16"), ("so", [128, 8], "uint16"),
                        ("tb", [128, 128], "float32"), ("cp", [128, 128], "float32"), ("ms", [128, 128], "float32"),
                        ("t16", [128, 8], "float32"), ("ta", [128, 8], "float32"), ("qa", [128, 8], "float32"), ("sg", [128, 8], "float32"),
                        ("zz", [128, 8], "float32"), ("ee", [128, 256], "bfloat16")):
@@ -66,21 +76,28 @@ for _h in range(2):
 DMAS = ["ld%d" % _k for _k in range(8)] + ["st%d" % _k for _k in range(4)]
 SEMAPHORES = ["V", "A", "P", "G", "sent"] + DMAS + ["%s%d%d" % (_a, _t, _h) for _a in ("al", "ab") for _t in (1, 2) for _h in (0, 1)]
 
-CY = 0.00083
-HOPT = 0.06
+COSTS = ({"cy": 0.00083, "V": 0.03, "A": 0.05, "P": 0.0005, "g": 1.5, "s": 3.8, "hop": 0.09},
+         {"cy": 0.00083, "V": 0.05, "A": 0.065, "P": 0.00075, "g": 1.5, "s": 3.8, "hop": 0.07},
+         {"cy": 0.00083, "V": 0.02, "A": 0.03, "P": 0.00042, "g": 1.3, "s": 3.0, "hop": 0.12},
+         {"cy": 0.00083, "V": 0.03, "A": 0.04, "P": 0.0005, "g": 1.9, "s": 5.0, "hop": 0.07})
 
 
-def cost(q, n):
-    if q == "V":
-        return 0.01 + max(64, n) * CY
-    if q == "A":
-        return 0.03 + max(64, n) * CY
+def cost(q, n, c):
+    if q not in ("A", "V", "P"):
+        return n
     if q == "P":
-        return n * 0.00042
-    return 0.2
+        return n * c["P"]
+    if isinstance(n, tuple):
+        return (0.065 if q == "A" else 0.05) + n[1] * c[n[0]] * c["cy"]
+    return c[q] + max(64, n) * c["cy"]
 
 
-def build(core, T, topo):
+CH = (2, 4, 2, 1)
+SPLIT = (0,)
+SEED, TRIES = 11, 12000
+
+
+def build(core, T, topo, VEC):
     ops, lastw, readers, banks = [], {}, {}, {}
 
     def add(q, fn, rd=(), wr=(), bk=(), c=0.1, sem=None, n=1, note=""):
@@ -106,17 +123,17 @@ def build(core, T, topo):
         for b in bk:
             banks.setdefault(b, {})[q] = me
         deps.discard(me)
-        ops.append({"q": q, "fn": fn, "deps": deps, "order": order - deps, "c": c, "sem": sem, "n": n, "note": note})
+        ops.append({"cls": 0, "q": q, "fn": fn, "deps": deps, "order": order - deps, "c": c, "sem": sem, "n": n, "note": note})
         return me
 
     def V(fn, rd, wr, n, bk=(), note=""):
-        return add("V", fn, rd, wr, bk, cost("V", n), note=note)
+        return add("V", fn, rd, wr, bk, n, note=note)
 
     def A(fn, rd, wr, n, bk=(), note=""):
-        return add("A", fn, rd, wr, bk, cost("A", n), note=note)
+        return add("A", fn, rd, wr, bk, n, note=note)
 
     def P(fn, rd, wr, n, bk=(), note=""):
-        return add("P", fn, rd, wr, bk, cost("P", n), note=note)
+        return add("P", fn, rd, wr, bk, n, note=note)
 
     def G(fn, rd, wr, c, note=""):
         return add("G", fn, rd, wr, (), c, note=note)
@@ -124,16 +141,24 @@ def build(core, T, topo):
     def load(q, k, out, in_, wr, c):
         add(q, lambda e: e.dma_start(out, in_), (), wr, (), c, sem="ld%d" % k, n=16, note="load")
 
-    gat = lambda n: int(60 + 1.5 * n)
+    gat = lambda n: ("g", n)
+
+    def gather_on(e, out, ind):
+        if e is VEC[0]:
+            return e.tensor_copy(out, ind)
+        return e.activation(out, ind, AF.Identity)
+
+    def either(fn, rd, wr, n, note):
+        add("AV", fn, rd, wr, (), n, note=note)
 
     load("Y", 0, T.bni[:, :, :], T.bn[:, :], ("bni",), 2.2)
     load("Q", 1, T.xw[:, 0:W], T.xf[:, :], ("xw",), 4.0)
     load("Y", 2, T.wti[:, :], T.wt[:, :], ("wti",), 2.5)
     load("Y", 3, T.thi[:, :], T.th[:, :], ("thi",), 2.5)
-    load("Y", 4, T.xw[:, W:2 * W], T.xf[:, :], ("xw2",), 6.0)
     load("Q", 5, T.cni[:, :], T.cn[:, :], ("cni",), 6.0)
 
     G(lambda e: e.iota(T.pi[:, 0:1], [[0, 1]], 0, 1), (), ("pi",), 0.2)
+    G(lambda e: e.iota(T.tu[:, :], [[16, 128]], 0, 1), (), ("tu",), 0.34)
     G(lambda e: e.iota(T.bli[:, :], [[0, 2], [1, 8]], 0, 0), (), ("bli",), 0.2)
     G(lambda e: e.iota(T.prow[:, :], [[0, 8], [1, 16]], 0, 0, allow_small_or_imprecise_dtypes=True), (), ("prow",), 0.4)
     V(lambda e: e.memset(T.ones[:, :], 1.0), (), ("ones",), 128)
@@ -154,18 +179,32 @@ def build(core, T, topo):
     def charts_in(h):
         V(lambda e: e.tensor_copy(T["bn0%d" % h][:, :], T.bni[:, 8 * h:8 * h + 8, :]), ("bni",), ("bn0%d" % h,), 128)
     lists_in(0)
+    V(lambda e: e.tensor_scalar(T.pj[:, 0:1], T.pi[:, 0:1], 15, None, OP.bitwise_and), ("pi",), ("pj",), 8)
+    V(lambda e: e.tensor_copy(T.icol[:, 0:1], T.pj[:, 0:1]), ("pj",), ("icol",), 8)
+    V(lambda e: e.tensor_tensor(T.wcol[:, 4:5], T.pi[:, 0:1], T.icol[:, 0:1], OP.subtract), ("pi", "icol"), ("p16",), 8)
+    V(lambda e: e.tensor_scalar(T.tv[:, :], T.tu[:, :], T.wcol[:, 4:5], None, OP.subtract), ("tu", "p16"), ("tv",), 128)
+    V(lambda e: e.tensor_scalar(T.tf[:, :], T.tv[:, :], 1184.0, None, OP.add), ("tv",), ("tf",), 128)
+    V(lambda e: e.tensor_tensor(T.tp[:, :], T.tv[:, :], T.tf[:, :], OP.mult), ("tv", "tf"), ("tp",), 256)
+    V(lambda e: e.tensor_scalar(T.tq[:, :], T.tp[:, :], 5, W - 1, OP.arith_shift_right, OP.bitwise_and), ("tp",), ("tq",), 128)
+    for l in range(4):
+        ls_ = slice(128 * l, 128 * l + 128)
+        V(lambda e, l=l, s=ls_: e.tensor_scalar(T.xa[:, s], T.tq[:, :], float(KAP[l] % W), None, OP.add), ("tq",), ("xa%d" % l,), 128)
+        V(lambda e, l=l, s=ls_: e.tensor_scalar(T.xb[:, s], T.xa[:, s], W - 1, None, OP.bitwise_and), ("xa%d" % l,), ("xb%d" % l,), 128)
+        V(lambda e, l=l, s=ls_: e.tensor_copy(T.xl[:, s], T.xb[:, s]), ("xb%d" % l,), ("xl%d" % l,), 128)
+        for c in range(4):
+            either(lambda e, l=l, c=c: gather_on(e, T.xt[:, W * l + 512 * c:W * l + 512 * c + 512], T.xw[:, :].indirect(T.xl[:, 128 * l + 32 * c:128 * l + 32 * c + 32])),
+                   ("xw", "xl%d" % l), ("x%d%d" % (l, c),), gat(512), "table")
     V(lambda e: e.tensor_scalar(T.nident[:, :], T.ident[:, :], -1.0, None, OP.mult), ("ident",), ("nident",), 64)
     V(lambda e: e.tensor_copy(T.wcol[:, 0:1], T.wti[:, :]), ("wti",), ("wcol",), 8)
     V(lambda e: e.tensor_scalar(T.zw[:, 15:128:16], T.bo[:, 0:128:16], T.wcol[:, 0:1], None, OP.mult), ("bo", "wcol"), ("zw",), 8)
     lists_in(1)
     V(lambda e: e.tensor_scalar(T.th16[:, 0:1], T.thi[:, :], 0.0625, None, OP.mult), ("thi",), ("th16",), 8)
-    V(lambda e: e.tensor_scalar(T.pj[:, 0:1], T.pi[:, 0:1], 15, None, OP.bitwise_and), ("pi",), ("pj",), 8)
-    V(lambda e: e.tensor_copy(T.icol[:, 0:1], T.pj[:, 0:1]), ("pj",), ("icol",), 8)
     V(lambda e: e.tensor_copy(T.bl[:, :], T.bli[:, :]), ("bli",), ("bl",), 16)
     V(lambda e: e.tensor_copy(T.z1[:, 15:128:16], T.bo[:, 0:128:16]), ("bo",), ("z1",), 8)
     V(lambda e: e.tensor_scalar(T.z16[:, 15:128:16], T.bo[:, 0:128:16], 0.0625, None, OP.mult), ("bo",), ("z16",), 8)
     V(lambda e: e.tensor_scalar(T.bow[:, :], T.bo[:, :], T.wcol[:, 0:1], None, OP.mult), ("bo", "wcol"), ("bow",), 64)
     V(lambda e: e.tensor_scalar(T.bo256[:, :], T.bo[:, :], 256.0, None, OP.mult), ("bo",), ("bo256",), 64)
+    V(lambda e: e.tensor_scalar(T.bo16[:, :], T.bo[:, :], T.icol[:, 0:1], 16.0, OP.mult, OP.mult), ("bo", "icol"), ("bo16",), 64)
     V(lambda e: e.memset(T.cmpc[:, 128:256], -0.25), (), ("cmpc",), 128)
     V(lambda e: e.tensor_scalar(T.cmpc[:, 0:128], T.prow[:, :], T.icol[:, 0:1], 0.25, OP.not_equal, OP.add), ("prow", "icol"), ("cmpc2",), 128)
     charts_in(0)
@@ -181,45 +220,61 @@ def build(core, T, topo):
         fa, dc, ac, ar = B("fa"), B("dc"), B("ac"), B("ar")
         zs = lambda z, i: z[:, 15 - i:143 - i]
 
+        def of(keys, c, ch):
+            return keys if ch == 1 or len(keys) == 1 else (keys[2 * c // ch],)
+
         def gather_pair(la, lb, ka, kb, n, w, wk, ch):
             m = n // ch
             for c in range(ch):
-                A(lambda e, c=c: e.activation(fa[:, m * c:m * c + m], w.indirect(la[:, m * c // 16:(m * c + m) // 16]), AF.Identity),
-                  ka + wk, (K("fa%d" % c),), gat(m), note="gA")
+                either(lambda e, c=c: gather_on(e, fa[:, m * c:m * c + m], w.indirect(la[:, m * c // 16:(m * c + m) // 16])),
+                       of(ka, c, ch) + wk, (K("fa%d" % c),), gat(m), "gA")
             for c in range(ch):
                 V(lambda e, c=c: e.tensor_tensor(dc[:, m * c:m * c + m], w.indirect(lb[:, m * c // 16:(m * c + m) // 16]), fa[:, m * c:m * c + m], OP.subtract),
-                  kb + wk + (K("fa%d" % c),), (K("dc%d" % c),), gat(m), note="gB")
+                  of(kb, c, ch) + wk + (K("fa%d" % c),), (K("dc%d" % c),), gat(m), note="gB")
             for c in range(ch):
                 A(lambda e, c=c: e.activation(ac[:, m * c:m * c + m], dc[:, m * c:m * c + m], AF.Abs), (K("dc%d" % c),), (K("ac%d" % c),), m, note="abs")
             return tuple(K("fa%d" % c) for c in range(ch)), tuple(K("dc%d" % c) for c in range(ch)), tuple(K("ac%d" % c) for c in range(ch))
 
-        def weigh(out, n, keys, wr):
-            def fn(e):
-                for i in range(16):
-                    o = e.matmul(out, zs(T.zw, i), ac[:, i:16 * n:16], i == 0, i == 15)
-                return o
-            P(fn, keys + ("zw",), wr, 16 * max(64, n), (K("S"),), note="weigh")
+        def weigh(l, n, keys):
+            for s, (c0, c1) in parts(l, n):
+                out = psum_of(s, c1 - c0)
+
+                def fn(e, out=out, c0=c0, c1=c1):
+                    for i in range(16):
+                        o = e.matmul(out, zs(T.zw, i), ac[:, 16 * c0 + i:16 * c1:16], i == 0, i == 15)
+                    return o
+                ch = len(keys)
+                ks = keys if ch == 1 or len(parts(l, n)) == 1 else keys[s * ch // 2:(s + 1) * ch // 2]
+                P(fn, ks + ("zw",), (K("S%d" % s),), 16 * max(64, c1 - c0), (K("S"),) if s == 0 else (K("F"),), note="weigh")
+
+        def parts(l, n):
+            return ((0, (0, n // 2)), (1, (n // 2, n))) if l in SPLIT else ((0, (0, n)),)
+
+        def psum_of(s, n):
+            return S[:, 0:n] if s == 0 else F[:, 256:256 + n]
 
         def index(l, n):
-            i1, i2, j = B("i1"), B("i2"), B("j%d" % l)
-            full = j[:, :, :]
-            V(lambda e: e.tensor_copy(i1[:, 0:n], S[:, 0:n]), (K("S"),), (K("i1"),), n, (K("S"),), note="i1")
-            V(lambda e: e.tensor_scalar(i2[:, 0:n], i1[:, 0:n], W - 1, None, OP.bitwise_and), (K("i1"),), (K("i2"),), n, note="i2")
-            V(lambda e: e.tensor_scalar(S[:, 256:256 + n], i2[:, 0:n], 1184.0, None, OP.add), (K("i2"),), (K("Su"),), n, (K("S"),), note="i3")
-            V(lambda e: e.tensor_tensor(i1[:, 0:n], i2[:, 0:n], S[:, 256:256 + n], OP.mult), (K("i2"), K("Su")), (K("i1"),), n, (K("S"),), note="i4")
-            V(lambda e: e.tensor_scalar(full, i1[:, 0:n], 5, W - 1, OP.arith_shift_right, OP.bitwise_and), (K("i1"),), (K("j"),), n, note="i5")
-            k = KAP[l] % W
-            r = k % 16
-            la, lb = B("la"), B("lb")
-            h2 = n // 2
-            m = n // 16
-            for x, (o, key) in enumerate(((la, "la"), (lb, "lb"))):
-                src = j[:, :, x * (m // 2):(x + 1) * (m // 2)] if l < 3 else j[:, x, :]
-                V(lambda e, o=o, src=src: e.tensor_scalar(o[:, 0:h2], src, float(r), None, OP.add), (K("j"),), (K(key),), h2, note="i6")
-            a = k - r
-            return T.xw[:, a:a + W + 16]
+            i1, j, m = B("i1"), B("j%d" % l), n // 16
+            for s, (c0, c1) in parts(l, n):
+                bank = (K("S"),) if s == 0 else (K("F"),)
+                src = psum_of(s, c1 - c0)
+                ks = (K("S%d" % s),)
+                V(lambda e, src=src, c0=c0, c1=c1: e.tensor_copy(i1[:, c0:c1], src), ks, (K("i1%d" % s),), c1 - c0, bank, note="i1")
+                rows_ = slice(c0 // m, c1 // m) if l < 3 else slice(c0 // 8, c1 // 8)
+                V(lambda e, c0=c0, c1=c1, rows_=rows_: e.tensor_scalar(j[:, rows_, :], i1[:, c0:c1], W - 1, None, OP.bitwise_and),
+                  (K("i1%d" % s),), (K("j%d" % s),), c1 - c0, note="i2")
+                for x, name in enumerate(("la", "lb")):
+                    if l == 3 and len(parts(l, n)) == 2 and x != s:
+                        continue
+                    wr = tuple(K("%s%d" % (name, y)) for y in ((0, 1) if l == 3 or len(parts(l, n)) == 1 else (s,)))
+                    if l < 3:
+                        V(lambda e, c0=c0, c1=c1, x=x, name=name, rows_=rows_: e.tensor_copy(B(name)[:, c0 // 2:c1 // 2], j[:, rows_, x * (m // 2):(x + 1) * (m // 2)]),
+                          (K("j%d" % s),), wr, (c1 - c0) // 2, note="i6")
+                    else:
+                        V(lambda e, x=x, name=name: e.tensor_copy(B(name)[:, 0:8], j[:, x, :]), (K("j%d" % s),), wr, 8, note="i6")
+            return T.xt[:, W * l:W * l + W], tuple("x%d%d" % (l, c) for c in range(4))
 
-        fk, dk, ak = gather_pair(lt[:, 0:64], lt[:, 64:128], ("lt%d%d0" % (t, h),), ("lt%d%d1" % (t, h),), 1024, win, ("xw",), 2)
+        fk, dk, ak = gather_pair(lt[:, 0:64], lt[:, 64:128], ("lt%d%d0" % (t, h),), ("lt%d%d1" % (t, h),), 1024, win, ("xw",), CH[0])
 
         def rows(bank, srcs):
             def fn(e):
@@ -233,40 +288,49 @@ def build(core, T, topo):
         P(rows(Y, (fa, dc)), fk + dk + ("ident", "nident"), (K("Y"),), 2048, (K("Y"),), note="row1")
         for ph, (bank, kk) in enumerate(((X, K("X")), (Y, K("Y")))):
             A(lambda e, ph=ph, bank=bank: e.activation(ar[:, ph, :, :], bank[:, :], AF.Abs), (kk,), (K("ar%d" % ph),), 512, (kk,), note="absr")
-        weigh(S[:, 0:64], 64, ak, (K("S"),))
+        sep = 0 in SPLIT
+        kr, br = (K("S1"), (K("F"),)) if sep else (K("S0"), (K("S"),))
+
+        def wcol(e):
+            for i in range(16):
+                o = e.matmul(S[:, 0:64], zs(T.zw, i), ac[:, i:1024:16], i == 0, i == 15)
+            return o
+        P(wcol, ak + ("zw",), (K("S0"),), 1024, (K("S"),), note="weigh")
 
         def wrow(e):
             for ph in range(2):
                 for pl in range(8):
-                    o = e.matmul(S[:, 64:128], zs(T.zw, 8 * ph + pl), ar[:, ph, :, 8 * pl:8 * pl + 8], ph + pl == 0, 8 * ph + pl == 15)
+                    o = e.matmul(psum_of(1, 64) if sep else S[:, 64:128], zs(T.zw, 8 * ph + pl), ar[:, ph, :, 8 * pl:8 * pl + 8], ph + pl == 0, 8 * ph + pl == 15)
             return o
-        P(wrow, ("zw", K("ar0"), K("ar1")), (K("S"),), 1024, (K("S"),), note="weighr")
-        w = index(0, 128)
+        P(wrow, ("zw", K("ar0"), K("ar1")), (kr,), 1024, br, note="weighr")
+        w, wk = index(0, 128)
         for l, n in ((1, 1024), (2, 512), (3, 256)):
-            fk, dk, ak = gather_pair(B("la"), B("lb"), (K("la"),), (K("lb"),), n, w, ("xw", "xw2"), 2 if n > 600 else 1)
-            weigh(S[:, 0:n // 16], n // 16, ak, (K("S"),))
-            w = index(l, n // 16)
+            fk, dk, ak = gather_pair(B("la"), B("lb"), (K("la0"), K("la1")), (K("lb0"), K("lb1")), n, w, wk, CH[l])
+            weigh(l, n // 16, ak)
+            w, wk = index(l, n // 16)
         wc, da, ii, id_ = B("wc"), B("da"), B("ii"), B("id")
-        wk = ("xw", "xw2")
-        A(lambda e: e.activation(wc[:, :], w.indirect(B("la")[:, 0:8]), AF.Identity), wk + (K("la"),), (K("wc"),), gat(128), note="gWC")
-        V(lambda e: e.tensor_tensor(da[:, 0, :], w.indirect(B("lb")[:, 0:8]), wc[:, :], OP.subtract), wk + (K("lb"), K("wc")), (K("dw"),), gat(128), note="gWR")
+        Fa, FaK = B("Y"), (K("Y"),)
+        A(lambda e: e.activation(wc[:, :], w.indirect(B("la")[:, 0:8]), AF.Identity), wk + (K("la0"),), (K("wc"),), gat(128), note="gWC")
+        V(lambda e: e.tensor_tensor(da[:, 0, :], w.indirect(B("lb")[:, 0:8]), wc[:, :], OP.subtract), wk + (K("lb0"), K("wc")), (K("dw"),), gat(128), note="gWR")
         A(lambda e: e.activation(da[:, 1, :], da[:, 0, :], AF.Abs), (K("dw"),), (K("aw"),), 128, note="absW")
         P(lambda e: e.matmul(F[:, 0:8], T.bow[:, :], wc[:, 0:128:16], True, True), (K("wc"), "bow"), (K("Fd"),), 64, (K("F"),), note="donor")
 
         def asum(e):
             for i in range(16):
-                o = e.matmul(F[:, 8:16], zs(T.z1, i), wc[:, i:128:16], i == 0, i == 15)
+                o = e.matmul(Fa[:, 48:56], zs(T.z1, i), wc[:, i:128:16], i == 0, i == 15)
             return o
-        P(asum, (K("wc"), "z1"), (K("Fa"),), 1024, (K("F"),), note="A")
-        V(lambda e: e.tensor_copy(ii[:, :], F[:, 0:16]), (K("Fd"), K("Fa")), (K("ii"),), 16, (K("F"),), note="f1")
-        V(lambda e: e.tensor_scalar(id_[:, :], ii[:, :], 15, None, OP.bitwise_and), (K("ii"),), (K("id"),), 16, note="f2")
+        P(asum, (K("wc"), "z1"), (K("Fa"),), 1024, FaK, note="A")
+        V(lambda e: e.tensor_copy(ii[:, 0:8], F[:, 0:8]), (K("Fd"),), (K("ii"),), 8, (K("F"),), note="f1")
+        V(lambda e: e.tensor_scalar(id_[:, 0:8], ii[:, 0:8], 15, None, OP.bitwise_and), (K("ii"),), (K("id"),), 8, note="f2")
+        V(lambda e: e.tensor_copy(ii[:, 8:16], Fa[:, 48:56]), (K("Fa"),), (K("iia"),), 8, FaK, note="f1a")
+        V(lambda e: e.tensor_scalar(id_[:, 8:16], ii[:, 8:16], 15, None, OP.bitwise_and), (K("iia"),), (K("ida"),), 8, note="f2a")
         V(lambda e: e.tensor_scalar(T.oh[:, 8 * h + 1:8 * h + 9], id_[:, 0:8], T.icol[:, 0:1], None, OP.is_equal), (K("id"), "icol"), ("oh%d" % h,), 8, note="oh")
         V(lambda e: e.tensor_tensor_scan(T.ex[:, 8 * h:8 * h + 8], T.oh[:, 8 * h:8 * h + 8], T.zero[:, 0:8], T.ex[:, 7:8] if h else 0.0, OP.add, OP.add),
           ("ohz", "oh0", "zero") + (("oh1", "ex0") if h else ()), ("ex%d" % h,), 8, note="scan")
         V(lambda e: e.tensor_tensor(B("ce")[:, :], T.oh[:, 8 * h + 1:8 * h + 9], T.ex[:, 8 * h:8 * h + 8], OP.mult), ("oh%d" % h, "ex%d" % h), (K("ce"),), 16, note="ce")
         P(lambda e: e.matmul(F[:, 32:40], T.bo256[:, :], B("ce")[:, :], True, True), (K("ce"), "bo256"), (K("Fc"),), 64, (K("F"),), note="cnt")
         V(lambda e: e.tensor_scalar(B("go")[:, :], id_[:, 0:8], 16.0, T.icol[:, 0:1], OP.mult, OP.add), (K("id"), "icol"), (K("go"),), 8, note="go")
-        V(lambda e: e.tensor_scalar(B("t16")[:, :], id_[:, 8:16], 0.0625, T.th16[:, 0:1], OP.mult, OP.add), (K("id"), "th16"), (K("t16"),), 8, note="t16")
+        V(lambda e: e.tensor_scalar(B("t16")[:, :], id_[:, 8:16], 0.0625, T.th16[:, 0:1], OP.mult, OP.add), (K("ida"), "th16"), (K("t16"),), 8, note="t16")
         V(lambda e: e.tensor_tensor(B("tb")[:, :], T.cw[:, 0:256].indirect(B("go")[:, :]), bn[:, :], OP.subtract), ("cw", K("go"), "bn%d%d" % (t, h)), (K("tb"),), gat(128), note="T")
         V(lambda e: e.tensor_tensor(B("ta")[:, :], B("t16")[:, :], F[:, 32:40], OP.add), (K("t16"), K("Fc")), (K("ta"),), 8, (K("F"),), note="ta")
 
@@ -285,10 +349,12 @@ def build(core, T, topo):
             return e.matmul(X[:, 0:128], T.ident[:, :], B("ee")[:, 128:256], False, True)
         P(xm, (K("ee"), "bo", "ident"), (K("X"),), 256, (K("X"),), note="X")
         A(lambda e: e.activation(Y[:, 0:128], X[:, 0:128], AF.Square, bias=-1.0), (K("X"),), (K("Y"),), 128, (K("X"), K("Y")), note="M")
-        V(lambda e: e.tensor_tensor(Y[:, 128:256], B("tb")[:, :], Y[:, 0:128], OP.mult), (K("tb"), K("Y")), (K("MT"),), 128, (K("Y"),), note="MT")
+        last = t == R - 1
         b3 = T["b3%d%d" % (t, h)]
         kb3 = "b3%d%d" % (t, h)
-        V(lambda e: e.tensor_tensor(b3[:, :, :], bn[:, :], Y[:, 128:256], OP.add), ("bn%d%d" % (t, h), K("MT")), (kb3,), 128, (K("Y"),), note="B")
+        mt = B("ms")[:, :] if last else Y[:, 128:256]
+        V(lambda e: e.tensor_tensor(mt, B("tb")[:, :], Y[:, 0:128], OP.mult), (K("tb"), K("Y")), (K("ms") if last else K("MT"),), 128, (K("Y"),), note="MT")
+        V(lambda e: e.tensor_tensor(b3[:, :, :], bn[:, :], mt, OP.add), ("bn%d%d" % (t, h), K("ms") if last else K("MT")), (kb3,), 256 if last else 128, () if last else (K("Y"),), note="B")
         if t < R - 1:
             ls = T["ls%d%d" % (t, h)]
             for ph in range(2):
@@ -305,21 +371,29 @@ def build(core, T, topo):
             ops[arr]["order"].add(o)
             o = add("G", lambda e: e.remote_dma(T["bn%d%d" % (t + 1, h)][:, :], b3[:, :, :], T.sem["ab%d%d" % (t + 1, h)], T.sem["sent"], pid, rid, mask),
                     (kb3,), (), (), 0.3, sem="-sent", n=ne, note="send2")
+            ops[o]["order"].add(arr - 1)
             arr = add(None, None, (), ("bn%d%d" % (t + 1, h),), (), 2.5, sem="ab%d%d" % (t + 1, h), n=ne)
             ops[arr]["order"].add(o)
         else:
             add("Y", lambda e: e.dma_start(T.yb[:, 128 * h:128 * h + 128], b3[:, :, :]), (kb3,), (), (), 2.0, sem="st%d" % h, n=16)
         A(lambda e: e.activation(B("cp")[:, :], T.cw[:, 0:256].indirect(B("go")[:, :]), AF.Identity), ("cw", K("go")), (K("cp"),), gat(128), note="CP")
-        A(lambda e: e.activation(B("ms")[:, :], Y[:, 128:256], AF.Identity), (K("MT"),), (K("ms"),), 128, (K("Y"),), note="MS")
-        V(lambda e: e.tensor_scalar(B("gf")[:, :], id_[:, 0:8], 16.0, T.icol[:, 0:1], OP.mult, OP.add), (K("id"), "icol"), (K("gf"),), 8, note="gf")
-        V(lambda e: e.tensor_tensor(B("sf")[:, :], B("gf")[:, :], F[:, 32:40], OP.add), (K("gf"), K("Fc")), (K("sf"),), 8, (K("F"),), note="sf")
-        V(lambda e: e.tensor_copy(B("so")[:, :], B("sf")[:, :]), (K("sf"),), (K("so"),), 8, note="so")
-        V(lambda e: e.tensor_tensor(T.cw[:, :].indirect(B("so")[:, :]), B("cp")[:, :], B("ms")[:, :], OP.subtract), (K("cp"), K("ms"), K("so")), ("cw",), 60 + 4 * 128, note="scatter")
+        if not last:
+            A(lambda e: e.activation(B("ms")[:, :], Y[:, 128:256], AF.Identity), (K("MT"),), (K("ms"),), 128, (K("Y"),), note="MS")
+
+        def smat(e):
+            e.matmul(F[:, 40:48], T.bo16[:, :], T.oh[:, 8 * h + 1:8 * h + 9], True, False)
+            return e.matmul(F[:, 40:48], T.bo256[:, :], B("ce")[:, :], False, True)
+        P(smat, (K("ce"), "oh%d" % h, "bo16", "bo256"), (K("Fs"),), 128, (K("F"),), note="so_p")
+        V(lambda e: e.tensor_scalar(B("so")[:, :], F[:, 40:48], T.icol[:, 0:1], None, OP.add), (K("Fs"), "icol"), (K("so"),), 8, (K("F"),), note="so")
+        V(lambda e: e.tensor_tensor(T.cw[:, :].indirect(B("so")[:, :]), B("cp")[:, :], B("ms")[:, :], OP.subtract), (K("cp"), K("ms"), K("so")), ("cw",), ("s", 128), note="scatter")
         V(lambda e: e.tensor_tensor(T["qr%d" % t][:, 8 * h:8 * h + 8], S[:, 392:400], B("t16")[:, :], OP.is_gt), (K("Sd"), K("t16")), ("qr%d%d" % (t, h),), 8, (K("S"),), note="qr")
 
     for t in range(R):
         for h in range(2):
+            k0 = len(ops)
             half(t, h)
+            for o in ops[k0:]:
+                o["cls"] = 2 * t + h
         if t == 1:
             V(lambda e: e.tensor_tensor(T.qs[:, :], T.qr0[:, :], T.qr1[:, :], OP.add), ("qr00", "qr01", "qr10", "qr11"), ("qs",), 32)
     V(lambda e: e.tensor_tensor(T.qf[:, :], T.qs[:, :], T.qr2[:, :], OP.add), ("qs", "qr20", "qr21"), ("qf",), 32)
@@ -328,39 +402,94 @@ def build(core, T, topo):
     return ops
 
 
-def schedule(ops):
+def schedule(ops, tries):
     n = len(ops)
-    tail = [0.0] * n
-    succ = [[] for _ in range(n)]
-    for i, o in enumerate(ops):
-        for d in o["deps"] | o["order"]:
-            succ[d].append(i)
+    c = [[{q: cost(q, o["c"], C) for q in (("A", "V") if o["q"] == "AV" else (o["q"],))} for o in ops] for C in COSTS]
+    deps = [(tuple(sorted(o["deps"])), tuple(sorted(o["order"]))) for o in ops]
+    succ, needs = [[] for _ in range(n)], [len(a) + len(b) for a, b in deps]
+    for i, (a, b) in enumerate(deps):
+        for d in a:
+            succ[d].append((i, COSTS[0]["hop"]))
+        for d in b:
+            succ[d].append((i, 0.0))
+    way = [0.0] * n
     for i in range(n - 1, -1, -1):
-        tail[i] = ops[i]["c"] + max([tail[s] + HOPT for s in succ[i]] or [0.0])
-    done, free, left, order, issued = {}, {}, set(range(n)), [], [False] * n
-    isq = lambda i: ops[i]["q"] in ("Y", "Q")
-    while left:
-        best = None
-        for i in left:
-            o = ops[i]
-            if any(d in left for d in o["deps"]) or any(d in left for d in o["order"]):
-                continue
-            r = 0.0
-            for d in o["deps"] | o["order"]:
-                r = max(r, done[d] + (HOPT if d in o["deps"] else 0.0))
-            if o["q"] is not None:
-                r = max(r, free.get(o["q"], 0.0))
-            key = (round(r, 3), -tail[i])
-            if best is None or key < best[0]:
-                best = (key, i, r)
-        _, i, r = best
-        o = ops[i]
-        left.discard(i)
-        done[i] = r + o["c"]
-        if o["q"] is not None:
-            free[o["q"]] = r + (0.06 if isq(i) else o["c"])
-        order.append(i)
-    return order, done
+        way[i] = min(c[0][i].values()) + max([way[s] + h for s, h in succ[i]] or [0.0])
+    first = [i for i in range(n) if needs[i] == 0]
+    free_to_choose = [i for i in range(n) if ops[i]["q"] == "AV"]
+
+    def listed(shift, pick):
+        rank = [s - w for s, w in zip(shift, way)]
+        est, free, order, need, ready, c0 = [0.0] * n, dict.fromkeys("AVPGYQ", 0.0), [], needs[:], first[:], c[0]
+        while ready:
+            b0, b1, bi = 1e9, 0.0, -1
+            for i in ready:
+                q = pick[i]
+                r = est[i]
+                if q is not None and free[q] > r:
+                    r = free[q]
+                if r < b0 - 0.005 or (r < b0 + 0.005 and rank[i] < b1):
+                    b0, b1, bi = r, rank[i], i
+            q = pick[bi]
+            r = est[bi] if q is None else max(est[bi], free[q])
+            ready.remove(bi)
+            order.append(bi)
+            x = c0[bi][q]
+            if q is not None:
+                free[q] = r + (0.06 if q in "YQ" else x)
+            for s, h in succ[bi]:
+                if r + x + h > est[s]:
+                    est[s] = r + x + h
+                need[s] -= 1
+                if need[s] == 0:
+                    ready.append(s)
+        return order
+
+    def spans(order, pick):
+        out = []
+        for C, cc in zip(COSTS, c):
+            hop, done, free = C["hop"], [0.0] * n, dict.fromkeys("AVPGYQ", 0.0)
+            for i in order:
+                r = 0.0
+                a, b = deps[i]
+                for d in a:
+                    if done[d] > r:
+                        r = done[d]
+                r = r + hop if a else r
+                for d in b:
+                    if done[d] > r:
+                        r = done[d]
+                q = pick[i]
+                x = cc[i][q]
+                if q is not None:
+                    if free[q] > r:
+                        r = free[q]
+                    free[q] = r + (0.06 if q in "YQ" else x)
+                done[i] = r + x
+            out.append(max(done))
+        return out, done
+
+    rng = np.random.default_rng(SEED)
+    shift, pick = [0.0] * n, ["A" if o["q"] == "AV" else o["q"] for o in ops]
+    order = listed(shift, pick)
+    base = spans(order, pick)[0]
+    cur, best = 1.0, (1.0, order, list(pick), base)
+    for k in range(tries):
+        s2, p2 = list(shift), list(pick)
+        for i in rng.integers(0, n, int(rng.choice([1, 2, 4, 10, 25]))):
+            s2[i] = float(4 * rng.normal())
+        if rng.random() < 0.3:
+            for i in rng.choice(free_to_choose, int(rng.integers(1, 3))):
+                p2[i] = "V" if p2[i] == "A" else "A"
+        order = listed(s2, p2)
+        sp = spans(order, p2)[0]
+        f = sum(a / b for a, b in zip(sp, base)) / len(sp)
+        if f < cur + 0.0004 * (1 - k / tries) * rng.random():
+            cur, shift, pick = f, s2, p2
+            if f < best[0]:
+                best = (f, order, p2, sp)
+    _, order, pick, sp = best
+    return order, spans(order, pick)[1], pick, (base, sp)
 
 
 _CACHE = {}
@@ -369,10 +498,12 @@ _CACHE = {}
 def rank_program(g, core, T, topo):
     if T.rank_of(core) is None:
         return
-    ops = build(core, T, topo)
+    ops = build(core, T, topo, [g.vector])
     if "order" not in _CACHE:
-        _CACHE["order"] = schedule(ops)
-    order, done = _CACHE["order"]
+        _CACHE["order"] = schedule(ops, TRIES)
+    order, done, pick, _ = _CACHE["order"]
+    for i, o in enumerate(ops):
+        o["q"] = pick[i]
     eng = {"V": g.vector, "A": g.scalar, "P": g.tensor, "G": g, "Y": g.sync, "Q": g.scalar}
     queue = {"V": "V", "A": "A", "Q": "A", "P": "P", "G": "G", "Y": "Y"}
     total, at, clock = {}, {}, {}

import numpy as np
from concourse.mybir import dt, AluOpType, AxisListType, ActivationFunctionType
import comms_topo

OP = AluOpType
AF = ActivationFunctionType
R, NB, HOP = 3, 16, 3
KAP = (101, 1303, 2717, 3911)
W = 2048

SCRATCH = {
    "xw": ("sbuf", [128, 2048], "bfloat16"),
    "tu": ("sbuf", [128, 128], "int32"),
    "tv": ("sbuf", [128, 128], "int32"),
    "tf": ("sbuf", [128, 128], "float32"),
    "tp": ("sbuf", [128, 128], "int32"),
    "tq": ("sbuf", [128, 128], "int32"),
    "bni": ("sbuf", [128, 16, 16], "int32"),
    "cni": ("sbuf", [128, 256], "int32"),
    "wti": ("sbuf", [128, 1], "int32"),
    "thi": ("sbuf", [128, 1], "int32"),
    "cw": ("sbuf", [128, 4096], "float32"),
    "pi": ("sbuf", [128, 8], "int32"),
    "pj": ("sbuf", [128, 8], "int32"),
    "icol": ("sbuf", [128, 8], "float32"),
    "wcol": ("sbuf", [128, 8], "float32"),
    "th16": ("sbuf", [128, 8], "float32"),
    "ones": ("sbuf", [128, 128], "bfloat16"),
    "m1": ("sbuf", [128, 128], "bfloat16"),
    "bo": ("sbuf", [128, 128], "bfloat16"),
    "bo256": ("sbuf", [128, 128], "bfloat16"),
    "bow": ("sbuf", [128, 128], "bfloat16"),
    "ident": ("sbuf", [128, 128], "bfloat16"),
    "nident": ("sbuf", [128, 128], "bfloat16"),
    "zw": ("sbuf", [128, 144], "bfloat16"),
    "z1": ("sbuf", [128, 144], "bfloat16"),
    "z16": ("sbuf", [128, 144], "bfloat16"),
    "prow": ("sbuf", [128, 128], "float32"),
    "cmpc": ("sbuf", [128, 256], "float32"),
    "bli": ("sbuf", [128, 16], "int32"),
    "bl": ("sbuf", [128, 16], "uint16"),
    "zero": ("sbuf", [128, 8], "float32"),
    "bo16": ("sbuf", [128, 128], "bfloat16"),
    "oh": ("sbuf", [128, 24], "bfloat16"),
    "ex": ("sbuf", [128, 16], "float32"),
    "qs": ("sbuf", [128, 16], "float32"),
    "qf": ("sbuf", [128, 16], "float32"),
}
SCRATCH["xt"] = ("sbuf", [128, 4 * W], "bfloat16")
SCRATCH["xa"] = ("sbuf", [128, 512], "int32")
SCRATCH["xb"] = ("sbuf", [128, 512], "int32")
SCRATCH["xl"] = ("sbuf", [128, 512], "uint16")
for _t in range(R):
    SCRATCH["qr%d" % _t] = ("sbuf", [128, 16], "float32")
    for _h in range(2):
        SCRATCH["lt%d%d" % (_t, _h)] = ("sbuf", [128, 128], "uint16")
        SCRATCH["bn%d%d" % (_t, _h)] = ("sbuf", [128, 128], "float32")
        SCRATCH["b3%d%d" % (_t, _h)] = ("sbuf", [128, 8, 16], "float32")
        if _t < R - 1:
            SCRATCH["ls%d%d" % (_t, _h)] = ("sbuf", [128, 128], "uint16")
for _h in range(2):
    for _n, _s, _d in (("fa", [128, 1024], "bfloat16"), ("dc", [128, 1024], "bfloat16"), ("ac", [128, 1024], "bfloat16"),
                       ("ar", [128, 2, 8, 64], "bfloat16"), ("i1", [128, 128], "int32"),
                       ("j0", [128, 16, 8], "int32"), ("j1", [128, 16, 4], "int32"), ("j2", [128, 16, 2], "int32"), ("j3", [128, 2, 8], "int32"),
                       ("la", [128, 64], "uint16"), ("lb", [128, 64], "uint16"),
                       ("wc", [128, 128], "bfloat16"), ("da", [128, 2, 128], "bfloat16"),
                       ("ii", [128, 16], "int32"), ("id", [128, 16], "int32"), ("ce", [128, 8], "bfloat16"),
                       ("go", [128, 8], "uint16"), ("so", [128, 8], "uint16"),
                       ("tb", [128, 128], "float32"), ("cp", [128, 128], "float32"), ("ms", [128, 128], "float32"),
                       ("t16", [128, 8], "float32"), ("ta", [128, 8], "float32"), ("qa", [128, 8], "float32"), ("sg", [128, 8], "float32"),
                       ("zz", [128, 8], "float32"), ("ee", [128, 256], "bfloat16")):
        SCRATCH["%s_%d" % (_n, _h)] = ("sbuf", _s, _d)
    for _n in ("S", "F", "X", "Y"):
        SCRATCH["%s_%d" % (_n, _h)] = ("psum", [128, 512], "float32")

DMAS = ["ld%d" % _k for _k in range(8)] + ["st%d" % _k for _k in range(4)]
SEMAPHORES = ["V", "A", "P", "G", "sent"] + DMAS + ["%s%d%d" % (_a, _t, _h) for _a in ("al", "ab") for _t in (1, 2) for _h in (0, 1)]

COSTS = ({"cy": 0.00083, "V": 0.03, "A": 0.05, "P": 0.0005, "g": 1.5, "s": 3.8, "hop": 0.09},
         {"cy": 0.00083, "V": 0.05, "A": 0.065, "P": 0.00075, "g": 1.5, "s": 3.8, "hop": 0.07},
         {"cy": 0.00083, "V": 0.02, "A": 0.03, "P": 0.00042, "g": 1.3, "s": 3.0, "hop": 0.12},
         {"cy": 0.00083, "V": 0.03, "A": 0.04, "P": 0.0005, "g": 1.9, "s": 5.0, "hop": 0.07})


def cost(q, n, c):
    if q not in ("A", "V", "P"):
        return n
    if q == "P":
        return n * c["P"]
    if isinstance(n, tuple):
        return (0.065 if q == "A" else 0.05) + n[1] * c[n[0]] * c["cy"]
    return c[q] + max(64, n) * c["cy"]


CH = (2, 4, 2, 1)
SPLIT = (0,)
SEED, TRIES = 11, 12000


def build(core, T, topo, VEC):
    ops, lastw, readers, banks = [], {}, {}, {}

    def add(q, fn, rd=(), wr=(), bk=(), c=0.1, sem=None, n=1, note=""):
        deps, order = set(), set()
        for k in rd:
            if k in lastw:
                deps.add(lastw[k])
        for k in wr:
            if k in lastw:
                deps.add(lastw[k])
            deps.update(readers.get(k, ()))
        for b in bk:
            for e, o in banks.get(b, {}).items():
                if e != q:
                    deps.add(o)
                else:
                    order.add(o)
        me = len(ops)
        for k in wr:
            lastw[k], readers[k] = me, []
        for k in rd:
            readers.setdefault(k, []).append(me)
        for b in bk:
            banks.setdefault(b, {})[q] = me
        deps.discard(me)
        ops.append({"cls": 0, "q": q, "fn": fn, "deps": deps, "order": order - deps, "c": c, "sem": sem, "n": n, "note": note})
        return me

    def V(fn, rd, wr, n, bk=(), note=""):
        return add("V", fn, rd, wr, bk, n, note=note)

    def A(fn, rd, wr, n, bk=(), note=""):
        return add("A", fn, rd, wr, bk, n, note=note)

    def P(fn, rd, wr, n, bk=(), note=""):
        return add("P", fn, rd, wr, bk, n, note=note)

    def G(fn, rd, wr, c, note=""):
        return add("G", fn, rd, wr, (), c, note=note)

    def load(q, k, out, in_, wr, c):
        add(q, lambda e: e.dma_start(out, in_), (), wr, (), c, sem="ld%d" % k, n=16, note="load")

    gat = lambda n: ("g", n)

    def gather_on(e, out, ind):
        if e is VEC[0]:
            return e.tensor_copy(out, ind)
        return e.activation(out, ind, AF.Identity)

    def either(fn, rd, wr, n, note):
        add("AV", fn, rd, wr, (), n, note=note)

    load("Y", 0, T.bni[:, :, :], T.bn[:, :], ("bni",), 2.2)
    load("Q", 1, T.xw[:, 0:W], T.xf[:, :], ("xw",), 4.0)
    load("Y", 2, T.wti[:, :], T.wt[:, :], ("wti",), 2.5)
    load("Y", 3, T.thi[:, :], T.th[:, :], ("thi",), 2.5)
    load("Q", 5, T.cni[:, :], T.cn[:, :], ("cni",), 6.0)

    G(lambda e: e.iota(T.pi[:, 0:1], [[0, 1]], 0, 1), (), ("pi",), 0.2)
    G(lambda e: e.iota(T.tu[:, :], [[16, 128]], 0, 1), (), ("tu",), 0.34)
    G(lambda e: e.iota(T.bli[:, :], [[0, 2], [1, 8]], 0, 0), (), ("bli",), 0.2)
    G(lambda e: e.iota(T.prow[:, :], [[0, 8], [1, 16]], 0, 0, allow_small_or_imprecise_dtypes=True), (), ("prow",), 0.4)
    V(lambda e: e.memset(T.ones[:, :], 1.0), (), ("ones",), 128)
    G(lambda e: e.affine_select(T.ident[:, :], T.ones[:, :], [[-1, 128]], OP.is_equal, 0.0, 0, 1), ("ones",), ("ident",), 0.4)
    G(lambda e: e.affine_select(T.m1[:, :], T.ones[:, :], [[-16, 8], [0, 16]], OP.is_ge, 0.0, 0, 1), ("ones",), ("m1",), 0.4)
    G(lambda e: e.affine_select(T.bo[:, :], T.m1[:, :], [[16, 8], [0, 16]], OP.is_ge, 0.0, 15, -1), ("m1",), ("bo",), 0.4)
    V(lambda e: e.memset(T.zw[:, :], 0.0), (), ("zw",), 144)
    V(lambda e: e.memset(T.z1[:, :], 0.0), (), ("z1",), 144)
    V(lambda e: e.memset(T.z16[:, :], 0.0), (), ("z16",), 144)
    V(lambda e: e.memset(T.zero[:, :], 0.0), (), ("zero",), 8)
    V(lambda e: e.memset(T.oh[:, 0:1], 0.0), (), ("ohz",), 8)

    def lists_in(h):
        for ph in range(2):
            V(lambda e, ph=ph: e.tensor_copy(T["lt0%d" % h][:, 64 * ph:64 * ph + 64], T.bni[:, 8 * h:8 * h + 8, 8 * ph:8 * ph + 8]),
              ("bni",), ("lt0%d%d" % (h, ph),), 64)

    def charts_in(h):
        V(lambda e: e.tensor_copy(T["bn0%d" % h][:, :], T.bni[:, 8 * h:8 * h + 8, :]), ("bni",), ("bn0%d" % h,), 128)
    lists_in(0)
    V(lambda e: e.tensor_scalar(T.pj[:, 0:1], T.pi[:, 0:1], 15, None, OP.bitwise_and), ("pi",), ("pj",), 8)
    V(lambda e: e.tensor_copy(T.icol[:, 0:1], T.pj[:, 0:1]), ("pj",), ("icol",), 8)
    V(lambda e: e.tensor_tensor(T.wcol[:, 4:5], T.pi[:, 0:1], T.icol[:, 0:1], OP.subtract), ("pi", "icol"), ("p16",), 8)
    V(lambda e: e.tensor_scalar(T.tv[:, :], T.tu[:, :], T.wcol[:, 4:5], None, OP.subtract), ("tu", "p16"), ("tv",), 128)
    V(lambda e: e.tensor_scalar(T.tf[:, :], T.tv[:, :], 1184.0, None, OP.add), ("tv",), ("tf",), 128)
    V(lambda e: e.tensor_tensor(T.tp[:, :], T.tv[:, :], T.tf[:, :], OP.mult), ("tv", "tf"), ("tp",), 256)
    V(lambda e: e.tensor_scalar(T.tq[:, :], T.tp[:, :], 5, W - 1, OP.arith_shift_right, OP.bitwise_and), ("tp",), ("tq",), 128)
    for l in range(4):
        ls_ = slice(128 * l, 128 * l + 128)
        V(lambda e, l=l, s=ls_: e.tensor_scalar(T.xa[:, s], T.tq[:, :], float(KAP[l] % W), None, OP.add), ("tq",), ("xa%d" % l,), 128)
        V(lambda e, l=l, s=ls_: e.tensor_scalar(T.xb[:, s], T.xa[:, s], W - 1, None, OP.bitwise_and), ("xa%d" % l,), ("xb%d" % l,), 128)
        V(lambda e, l=l, s=ls_: e.tensor_copy(T.xl[:, s], T.xb[:, s]), ("xb%d" % l,), ("xl%d" % l,), 128)
        for c in range(4):
            either(lambda e, l=l, c=c: gather_on(e, T.xt[:, W * l + 512 * c:W * l + 512 * c + 512], T.xw[:, :].indirect(T.xl[:, 128 * l + 32 * c:128 * l + 32 * c + 32])),
                   ("xw", "xl%d" % l), ("x%d%d" % (l, c),), gat(512), "table")
    V(lambda e: e.tensor_scalar(T.nident[:, :], T.ident[:, :], -1.0, None, OP.mult), ("ident",), ("nident",), 64)
    V(lambda e: e.tensor_copy(T.wcol[:, 0:1], T.wti[:, :]), ("wti",), ("wcol",), 8)
    V(lambda e: e.tensor_scalar(T.zw[:, 15:128:16], T.bo[:, 0:128:16], T.wcol[:, 0:1], None, OP.mult), ("bo", "wcol"), ("zw",), 8)
    lists_in(1)
    V(lambda e: e.tensor_scalar(T.th16[:, 0:1], T.thi[:, :], 0.0625, None, OP.mult), ("thi",), ("th16",), 8)
    V(lambda e: e.tensor_copy(T.bl[:, :], T.bli[:, :]), ("bli",), ("bl",), 16)
    V(lambda e: e.tensor_copy(T.z1[:, 15:128:16], T.bo[:, 0:128:16]), ("bo",), ("z1",), 8)
    V(lambda e: e.tensor_scalar(T.z16[:, 15:128:16], T.bo[:, 0:128:16], 0.0625, None, OP.mult), ("bo",), ("z16",), 8)
    V(lambda e: e.tensor_scalar(T.bow[:, :], T.bo[:, :], T.wcol[:, 0:1], None, OP.mult), ("bo", "wcol"), ("bow",), 64)
    V(lambda e: e.tensor_scalar(T.bo256[:, :], T.bo[:, :], 256.0, None, OP.mult), ("bo",), ("bo256",), 64)
    V(lambda e: e.tensor_scalar(T.bo16[:, :], T.bo[:, :], T.icol[:, 0:1], 16.0, OP.mult, OP.mult), ("bo", "icol"), ("bo16",), 64)
    V(lambda e: e.memset(T.cmpc[:, 128:256], -0.25), (), ("cmpc",), 128)
    V(lambda e: e.tensor_scalar(T.cmpc[:, 0:128], T.prow[:, :], T.icol[:, 0:1], 0.25, OP.not_equal, OP.add), ("prow", "icol"), ("cmpc2",), 128)
    charts_in(0)
    charts_in(1)
    V(lambda e: e.tensor_copy(T.cw[:, 0:256], T.cni[:, :]), ("cni",), ("cw",), 256)

    def half(t, h):
        B = lambda n: T["%s_%d" % (n, h)]
        K = lambda n: "%s_%d" % (n, h)
        S, F, X, Y = B("S"), B("F"), B("X"), B("Y")
        lt, bn = T["lt%d%d" % (t, h)], T["bn%d%d" % (t, h)]
        win = T.xw[:, 0:W]
        fa, dc, ac, ar = B("fa"), B("dc"), B("ac"), B("ar")
        zs = lambda z, i: z[:, 15 - i:143 - i]

        def of(keys, c, ch):
            return keys if ch == 1 or len(keys) == 1 else (keys[2 * c // ch],)

        def gather_pair(la, lb, ka, kb, n, w, wk, ch):
            m = n // ch
            for c in range(ch):
                either(lambda e, c=c: gather_on(e, fa[:, m * c:m * c + m], w.indirect(la[:, m * c // 16:(m * c + m) // 16])),
                       of(ka, c, ch) + wk, (K("fa%d" % c),), gat(m), "gA")
            for c in range(ch):
                V(lambda e, c=c: e.tensor_tensor(dc[:, m * c:m * c + m], w.indirect(lb[:, m * c // 16:(m * c + m) // 16]), fa[:, m * c:m * c + m], OP.subtract),
                  of(kb, c, ch) + wk + (K("fa%d" % c),), (K("dc%d" % c),), gat(m), note="gB")
            for c in range(ch):
                A(lambda e, c=c: e.activation(ac[:, m * c:m * c + m], dc[:, m * c:m * c + m], AF.Abs), (K("dc%d" % c),), (K("ac%d" % c),), m, note="abs")
            return tuple(K("fa%d" % c) for c in range(ch)), tuple(K("dc%d" % c) for c in range(ch)), tuple(K("ac%d" % c) for c in range(ch))

        def weigh(l, n, keys):
            for s, (c0, c1) in parts(l, n):
                out = psum_of(s, c1 - c0)

                def fn(e, out=out, c0=c0, c1=c1):
                    for i in range(16):
                        o = e.matmul(out, zs(T.zw, i), ac[:, 16 * c0 + i:16 * c1:16], i == 0, i == 15)
                    return o
                ch = len(keys)
                ks = keys if ch == 1 or len(parts(l, n)) == 1 else keys[s * ch // 2:(s + 1) * ch // 2]
                P(fn, ks + ("zw",), (K("S%d" % s),), 16 * max(64, c1 - c0), (K("S"),) if s == 0 else (K("F"),), note="weigh")

        def parts(l, n):
            return ((0, (0, n // 2)), (1, (n // 2, n))) if l in SPLIT else ((0, (0, n)),)

        def psum_of(s, n):
            return S[:, 0:n] if s == 0 else F[:, 256:256 + n]

        def index(l, n):
            i1, j, m = B("i1"), B("j%d" % l), n // 16
            for s, (c0, c1) in parts(l, n):
                bank = (K("S"),) if s == 0 else (K("F"),)
                src = psum_of(s, c1 - c0)
                ks = (K("S%d" % s),)
                V(lambda e, src=src, c0=c0, c1=c1: e.tensor_copy(i1[:, c0:c1], src), ks, (K("i1%d" % s),), c1 - c0, bank, note="i1")
                rows_ = slice(c0 // m, c1 // m) if l < 3 else slice(c0 // 8, c1 // 8)
                V(lambda e, c0=c0, c1=c1, rows_=rows_: e.tensor_scalar(j[:, rows_, :], i1[:, c0:c1], W - 1, None, OP.bitwise_and),
                  (K("i1%d" % s),), (K("j%d" % s),), c1 - c0, note="i2")
                for x, name in enumerate(("la", "lb")):
                    if l == 3 and len(parts(l, n)) == 2 and x != s:
                        continue
                    wr = tuple(K("%s%d" % (name, y)) for y in ((0, 1) if l == 3 or len(parts(l, n)) == 1 else (s,)))
                    if l < 3:
                        V(lambda e, c0=c0, c1=c1, x=x, name=name, rows_=rows_: e.tensor_copy(B(name)[:, c0 // 2:c1 // 2], j[:, rows_, x * (m // 2):(x + 1) * (m // 2)]),
                          (K("j%d" % s),), wr, (c1 - c0) // 2, note="i6")
                    else:
                        V(lambda e, x=x, name=name: e.tensor_copy(B(name)[:, 0:8], j[:, x, :]), (K("j%d" % s),), wr, 8, note="i6")
            return T.xt[:, W * l:W * l + W], tuple("x%d%d" % (l, c) for c in range(4))

        fk, dk, ak = gather_pair(lt[:, 0:64], lt[:, 64:128], ("lt%d%d0" % (t, h),), ("lt%d%d1" % (t, h),), 1024, win, ("xw",), CH[0])

        def rows(bank, srcs):
            def fn(e):
                for c in range(8):
                    lst = [(T.ident, s[:, c:1024:16]) for s in srcs] + [(T.nident, s[:, c + 8:1024:16]) for s in srcs]
                    for i, (w, r) in enumerate(lst):
                        o = e.matmul(bank[:, c:512:8], w[:, :], r, i == 0, i == len(lst) - 1)
                return o
            return fn
        P(rows(X, (fa,)), fk + ("ident", "nident"), (K("X"),), 1024, (K("X"),), note="row0")
        P(rows(Y, (fa, dc)), fk + dk + ("ident", "nident"), (K("Y"),), 2048, (K("Y"),), note="row1")
        for ph, (bank, kk) in enumerate(((X, K("X")), (Y, K("Y")))):
            A(lambda e, ph=ph, bank=bank: e.activation(ar[:, ph, :, :], bank[:, :], AF.Abs), (kk,), (K("ar%d" % ph),), 512, (kk,), note="absr")
        sep = 0 in SPLIT
        kr, br = (K("S1"), (K("F"),)) if sep else (K("S0"), (K("S"),))

        def wcol(e):
            for i in range(16):
                o = e.matmul(S[:, 0:64], zs(T.zw, i), ac[:, i:1024:16], i == 0, i == 15)
            return o
        P(wcol, ak + ("zw",), (K("S0"),), 1024, (K("S"),), note="weigh")

        def wrow(e):
            for ph in range(2):
                for pl in range(8):
                    o = e.matmul(psum_of(1, 64) if sep else S[:, 64:128], zs(T.zw, 8 * ph + pl), ar[:, ph, :, 8 * pl:8 * pl + 8], ph + pl == 0, 8 * ph + pl == 15)
            return o
        P(wrow, ("zw", K("ar0"), K("ar1")), (kr,), 1024, br, note="weighr")
        w, wk = index(0, 128)
        for l, n in ((1, 1024), (2, 512), (3, 256)):
            fk, dk, ak = gather_pair(B("la"), B("lb"), (K("la0"), K("la1")), (K("lb0"), K("lb1")), n, w, wk, CH[l])
            weigh(l, n // 16, ak)
            w, wk = index(l, n // 16)
        wc, da, ii, id_ = B("wc"), B("da"), B("ii"), B("id")
        Fa, FaK = B("Y"), (K("Y"),)
        A(lambda e: e.activation(wc[:, :], w.indirect(B("la")[:, 0:8]), AF.Identity), wk + (K("la0"),), (K("wc"),), gat(128), note="gWC")
        V(lambda e: e.tensor_tensor(da[:, 0, :], w.indirect(B("lb")[:, 0:8]), wc[:, :], OP.subtract), wk + (K("lb0"), K("wc")), (K("dw"),), gat(128), note="gWR")
        A(lambda e: e.activation(da[:, 1, :], da[:, 0, :], AF.Abs), (K("dw"),), (K("aw"),), 128, note="absW")
        P(lambda e: e.matmul(F[:, 0:8], T.bow[:, :], wc[:, 0:128:16], True, True), (K("wc"), "bow"), (K("Fd"),), 64, (K("F"),), note="donor")

        def asum(e):
            for i in range(16):
                o = e.matmul(Fa[:, 48:56], zs(T.z1, i), wc[:, i:128:16], i == 0, i == 15)
            return o
        P(asum, (K("wc"), "z1"), (K("Fa"),), 1024, FaK, note="A")
        V(lambda e: e.tensor_copy(ii[:, 0:8], F[:, 0:8]), (K("Fd"),), (K("ii"),), 8, (K("F"),), note="f1")
        V(lambda e: e.tensor_scalar(id_[:, 0:8], ii[:, 0:8], 15, None, OP.bitwise_and), (K("ii"),), (K("id"),), 8, note="f2")
        V(lambda e: e.tensor_copy(ii[:, 8:16], Fa[:, 48:56]), (K("Fa"),), (K("iia"),), 8, FaK, note="f1a")
        V(lambda e: e.tensor_scalar(id_[:, 8:16], ii[:, 8:16], 15, None, OP.bitwise_and), (K("iia"),), (K("ida"),), 8, note="f2a")
        V(lambda e: e.tensor_scalar(T.oh[:, 8 * h + 1:8 * h + 9], id_[:, 0:8], T.icol[:, 0:1], None, OP.is_equal), (K("id"), "icol"), ("oh%d" % h,), 8, note="oh")
        V(lambda e: e.tensor_tensor_scan(T.ex[:, 8 * h:8 * h + 8], T.oh[:, 8 * h:8 * h + 8], T.zero[:, 0:8], T.ex[:, 7:8] if h else 0.0, OP.add, OP.add),
          ("ohz", "oh0", "zero") + (("oh1", "ex0") if h else ()), ("ex%d" % h,), 8, note="scan")
        V(lambda e: e.tensor_tensor(B("ce")[:, :], T.oh[:, 8 * h + 1:8 * h + 9], T.ex[:, 8 * h:8 * h + 8], OP.mult), ("oh%d" % h, "ex%d" % h), (K("ce"),), 16, note="ce")
        P(lambda e: e.matmul(F[:, 32:40], T.bo256[:, :], B("ce")[:, :], True, True), (K("ce"), "bo256"), (K("Fc"),), 64, (K("F"),), note="cnt")
        V(lambda e: e.tensor_scalar(B("go")[:, :], id_[:, 0:8], 16.0, T.icol[:, 0:1], OP.mult, OP.add), (K("id"), "icol"), (K("go"),), 8, note="go")
        V(lambda e: e.tensor_scalar(B("t16")[:, :], id_[:, 8:16], 0.0625, T.th16[:, 0:1], OP.mult, OP.add), (K("ida"), "th16"), (K("t16"),), 8, note="t16")
        V(lambda e: e.tensor_tensor(B("tb")[:, :], T.cw[:, 0:256].indirect(B("go")[:, :]), bn[:, :], OP.subtract), ("cw", K("go"), "bn%d%d" % (t, h)), (K("tb"),), gat(128), note="T")
        V(lambda e: e.tensor_tensor(B("ta")[:, :], B("t16")[:, :], F[:, 32:40], OP.add), (K("t16"), K("Fc")), (K("ta"),), 8, (K("F"),), note="ta")

        def dsum(e):
            for i in range(16):
                o = e.matmul(S[:, 384:400], zs(T.z16, i), da[:, :, i:128:16], i == 0, i == 15)
            return o
        P(dsum, (K("dw"), K("aw"), "z16"), (K("Sd"),), 1024, (K("S"),), note="D")
        V(lambda e: e.tensor_scalar(B("sg")[:, :], S[:, 384:392], 0.0, 0.5, OP.is_lt, OP.subtract), (K("Sd"),), (K("sg"),), 8, (K("S"),), note="sg")
        V(lambda e: e.tensor_tensor(B("qa")[:, :], S[:, 392:400], B("ta")[:, :], OP.is_gt), (K("Sd"), K("ta")), (K("qa"),), 8, (K("S"),), note="qa")
        V(lambda e: e.tensor_tensor(B("zz")[:, :], B("sg")[:, :], B("qa")[:, :], OP.mult), (K("sg"), K("qa")), (K("zz"),), 16, note="zz")
        V(lambda e: e.tensor_tensor(B("ee")[:, :], B("zz")[:, 0:8].indirect(T.bl[:, :]), T.cmpc[:, :], OP.is_ge), (K("zz"), "bl", "cmpc", "cmpc2"), (K("ee"),), gat(256), note="ee")

        def xm(e):
            e.matmul(X[:, 0:128], T.bo[:, :], B("ee")[:, 0:128], True, False)
            return e.matmul(X[:, 0:128], T.ident[:, :], B("ee")[:, 128:256], False, True)
        P(xm, (K("ee"), "bo", "ident"), (K("X"),), 256, (K("X"),), note="X")
        A(lambda e: e.activation(Y[:, 0:128], X[:, 0:128], AF.Square, bias=-1.0), (K("X"),), (K("Y"),), 128, (K("X"), K("Y")), note="M")
        last = t == R - 1
        b3 = T["b3%d%d" % (t, h)]
        kb3 = "b3%d%d" % (t, h)
        mt = B("ms")[:, :] if last else Y[:, 128:256]
        V(lambda e: e.tensor_tensor(mt, B("tb")[:, :], Y[:, 0:128], OP.mult), (K("tb"), K("Y")), (K("ms") if last else K("MT"),), 128, (K("Y"),), note="MT")
        V(lambda e: e.tensor_tensor(b3[:, :, :], bn[:, :], mt, OP.add), ("bn%d%d" % (t, h), K("ms") if last else K("MT")), (kb3,), 256 if last else 128, () if last else (K("Y"),), note="B")
        if t < R - 1:
            ls = T["ls%d%d" % (t, h)]
            for ph in range(2):
                V(lambda e, ph=ph: e.tensor_copy(ls[:, 64 * ph:64 * ph + 64], b3[:, :, 8 * ph:8 * ph + 8]), (kb3,), ("ls%d%d%d" % (t, h, ph),), 64, note="ls")
            dst = T.cores[(T.rank_of(core) + HOP) % len(T.cores)]
            rid, pid, _ = topo.addr(dst)
            mask = 0
            for en in topo.engines(core, dst)[::2]:
                mask |= 1 << en
            ne = len(topo.engines(core, dst)[::2])
            o = add("G", lambda e: e.remote_dma(T["lt%d%d" % (t + 1, h)][:, :], ls[:, :], T.sem["al%d%d" % (t + 1, h)], T.sem["sent"], pid, rid, mask),
                    ("ls%d%d0" % (t, h), "ls%d%d1" % (t, h)), (), (), 0.3, sem="-sent", n=ne, note="send")
            arr = add(None, None, (), ("lt%d%d0" % (t + 1, h), "lt%d%d1" % (t + 1, h)), (), 2.0, sem="al%d%d" % (t + 1, h), n=ne)
            ops[arr]["order"].add(o)
            o = add("G", lambda e: e.remote_dma(T["bn%d%d" % (t + 1, h)][:, :], b3[:, :, :], T.sem["ab%d%d" % (t + 1, h)], T.sem["sent"], pid, rid, mask),
                    (kb3,), (), (), 0.3, sem="-sent", n=ne, note="send2")
            ops[o]["order"].add(arr - 1)
            arr = add(None, None, (), ("bn%d%d" % (t + 1, h),), (), 2.5, sem="ab%d%d" % (t + 1, h), n=ne)
            ops[arr]["order"].add(o)
        else:
            add("Y", lambda e: e.dma_start(T.yb[:, 128 * h:128 * h + 128], b3[:, :, :]), (kb3,), (), (), 2.0, sem="st%d" % h, n=16)
        A(lambda e: e.activation(B("cp")[:, :], T.cw[:, 0:256].indirect(B("go")[:, :]), AF.Identity), ("cw", K("go")), (K("cp"),), gat(128), note="CP")
        if not last:
            A(lambda e: e.activation(B("ms")[:, :], Y[:, 128:256], AF.Identity), (K("MT"),), (K("ms"),), 128, (K("Y"),), note="MS")

        def smat(e):
            e.matmul(F[:, 40:48], T.bo16[:, :], T.oh[:, 8 * h + 1:8 * h + 9], True, False)
            return e.matmul(F[:, 40:48], T.bo256[:, :], B("ce")[:, :], False, True)
        P(smat, (K("ce"), "oh%d" % h, "bo16", "bo256"), (K("Fs"),), 128, (K("F"),), note="so_p")
        V(lambda e: e.tensor_scalar(B("so")[:, :], F[:, 40:48], T.icol[:, 0:1], None, OP.add), (K("Fs"), "icol"), (K("so"),), 8, (K("F"),), note="so")
        V(lambda e: e.tensor_tensor(T.cw[:, :].indirect(B("so")[:, :]), B("cp")[:, :], B("ms")[:, :], OP.subtract), (K("cp"), K("ms"), K("so")), ("cw",), ("s", 128), note="scatter")
        V(lambda e: e.tensor_tensor(T["qr%d" % t][:, 8 * h:8 * h + 8], S[:, 392:400], B("t16")[:, :], OP.is_gt), (K("Sd"), K("t16")), ("qr%d%d" % (t, h),), 8, (K("S"),), note="qr")

    for t in range(R):
        for h in range(2):
            k0 = len(ops)
            half(t, h)
            for o in ops[k0:]:
                o["cls"] = 2 * t + h
        if t == 1:
            V(lambda e: e.tensor_tensor(T.qs[:, :], T.qr0[:, :], T.qr1[:, :], OP.add), ("qr00", "qr01", "qr10", "qr11"), ("qs",), 32)
    V(lambda e: e.tensor_tensor(T.qf[:, :], T.qs[:, :], T.qr2[:, :], OP.add), ("qs", "qr20", "qr21"), ("qf",), 32)
    add("Y", lambda e: e.dma_start(T.yq[:, :], T.qf[:, :]), ("qf",), (), (), 2.0, sem="st2", n=16)
    add("Q", lambda e: e.dma_start(T.yc[:, :], T.cw[:, 0:256]), ("cw",), (), (), 2.0, sem="st3", n=16)
    return ops


def schedule(ops, tries):
    n = len(ops)
    c = [[{q: cost(q, o["c"], C) for q in (("A", "V") if o["q"] == "AV" else (o["q"],))} for o in ops] for C in COSTS]
    deps = [(tuple(sorted(o["deps"])), tuple(sorted(o["order"]))) for o in ops]
    succ, needs = [[] for _ in range(n)], [len(a) + len(b) for a, b in deps]
    for i, (a, b) in enumerate(deps):
        for d in a:
            succ[d].append((i, COSTS[0]["hop"]))
        for d in b:
            succ[d].append((i, 0.0))
    way = [0.0] * n
    for i in range(n - 1, -1, -1):
        way[i] = min(c[0][i].values()) + max([way[s] + h for s, h in succ[i]] or [0.0])
    first = [i for i in range(n) if needs[i] == 0]
    free_to_choose = [i for i in range(n) if ops[i]["q"] == "AV"]

    def listed(shift, pick):
        rank = [s - w for s, w in zip(shift, way)]
        est, free, order, need, ready, c0 = [0.0] * n, dict.fromkeys("AVPGYQ", 0.0), [], needs[:], first[:], c[0]
        while ready:
            b0, b1, bi = 1e9, 0.0, -1
            for i in ready:
                q = pick[i]
                r = est[i]
                if q is not None and free[q] > r:
                    r = free[q]
                if r < b0 - 0.005 or (r < b0 + 0.005 and rank[i] < b1):
                    b0, b1, bi = r, rank[i], i
            q = pick[bi]
            r = est[bi] if q is None else max(est[bi], free[q])
            ready.remove(bi)
            order.append(bi)
            x = c0[bi][q]
            if q is not None:
                free[q] = r + (0.06 if q in "YQ" else x)
            for s, h in succ[bi]:
                if r + x + h > est[s]:
                    est[s] = r + x + h
                need[s] -= 1
                if need[s] == 0:
                    ready.append(s)
        return order

    def spans(order, pick):
        out = []
        for C, cc in zip(COSTS, c):
            hop, done, free = C["hop"], [0.0] * n, dict.fromkeys("AVPGYQ", 0.0)
            for i in order:
                r = 0.0
                a, b = deps[i]
                for d in a:
                    if done[d] > r:
                        r = done[d]
                r = r + hop if a else r
                for d in b:
                    if done[d] > r:
                        r = done[d]
                q = pick[i]
                x = cc[i][q]
                if q is not None:
                    if free[q] > r:
                        r = free[q]
                    free[q] = r + (0.06 if q in "YQ" else x)
                done[i] = r + x
            out.append(max(done))
        return out, done

    rng = np.random.default_rng(SEED)
    shift, pick = [0.0] * n, ["A" if o["q"] == "AV" else o["q"] for o in ops]
    order = listed(shift, pick)
    base = spans(order, pick)[0]
    cur, best = 1.0, (1.0, order, list(pick), base)
    for k in range(tries):
        s2, p2 = list(shift), list(pick)
        for i in rng.integers(0, n, int(rng.choice([1, 2, 4, 10, 25]))):
            s2[i] = float(4 * rng.normal())
        if rng.random() < 0.3:
            for i in rng.choice(free_to_choose, int(rng.integers(1, 3))):
                p2[i] = "V" if p2[i] == "A" else "A"
        order = listed(s2, p2)
        sp = spans(order, p2)[0]
        f = sum(a / b for a, b in zip(sp, base)) / len(sp)
        if f < cur + 0.0004 * (1 - k / tries) * rng.random():
            cur, shift, pick = f, s2, p2
            if f < best[0]:
                best = (f, order, p2, sp)
    _, order, pick, sp = best
    return order, spans(order, pick)[1], pick, (base, sp)


_CACHE = {}


def rank_program(g, core, T, topo):
    if T.rank_of(core) is None:
        return
    ops = build(core, T, topo, [g.vector])
    if "order" not in _CACHE:
        _CACHE["order"] = schedule(ops, TRIES)
    order, done, pick, _ = _CACHE["order"]
    for i, o in enumerate(ops):
        o["q"] = pick[i]
    eng = {"V": g.vector, "A": g.scalar, "P": g.tensor, "G": g, "Y": g.sync, "Q": g.scalar}
    queue = {"V": "V", "A": "A", "Q": "A", "P": "P", "G": "G", "Y": "Y"}
    total, at, clock = {}, {}, {}
    known = {q: {} for q in ("V", "A", "P", "G", "Y")}
    for i in order:
        o = ops[i]
        if o["q"] is None:
            at[i] = (o["sem"], o["n"])
            clock[i] = {o["sem"]: o["n"]}
            continue
        qn = queue[o["q"]]
        e = eng[o["q"]]
        kn = known[qn]
        for d in sorted(o["deps"], key=lambda d: -done[d]):
            s, c = at[d]
            if kn.get(s, 0) < c:
                e.wait_ge(T.sem[s], c)
                for s2, c2 in clock[d].items():
                    kn[s2] = max(kn.get(s2, 0), c2)
        ins = o["fn"](e)
        if o["sem"] is None:
            s, n = o["q"], 1
            total[s] = total.get(s, 0) + n
            ins.then_inc(T.sem[s], n)
        elif o["sem"] == "-sent":
            s = "sent"
            total[s] = total.get(s, 0) + o["n"]
        else:
            s, n = o["sem"], o["n"]
            total[s] = total.get(s, 0) + n
            ins.then_inc(T.sem[s], n)
        at[i] = (s, total[s])
        clock[i] = dict(kn)
        clock[i][s] = total[s]
    for s, c in total.items():
        if known["G"].get(s, 0) < c:
            g.wait_ge(T.sem[s], c)
